import numpy as np
import ml_dtypes


def mxq(x, axis, fmt="e4m3"):
    dtype, down = {"e4m3": (ml_dtypes.float8_e4m3fn, 7), "e5m2": (ml_dtypes.float8_e5m2, 14)}[fmt]
    v = np.moveaxis(np.asarray(x, np.float32).astype(ml_dtypes.bfloat16).astype(np.float64), axis, -1)
    blocks = v.reshape(v.shape[:-1] + (-1, 32))
    amax = np.abs(blocks).max(-1, keepdims=True)
    byte = np.maximum(np.where(amax > 0, np.frexp(amax)[1] - 1 + 127, 0) - down, 1)
    scale = np.exp2(byte - 127.0)
    codes = (blocks / scale).astype(np.float32).astype(dtype).astype(np.float64)
    return np.moveaxis((codes * scale).reshape(v.shape), -1, axis)


WIDE = False


def mx_kscale(k):
    if not WIDE:
        return np.ones(k)
    levels = np.array([10, -10, 5, -5, 0])
    if k % 512:
        return np.exp2(np.random.permutation(np.resize(levels, k // 32))).repeat(32)
    a = np.empty((k // 512, 16))
    for p in range(k // 512):
        a[p, :8] = np.random.permutation(np.resize(levels, 8))
        for g in range(8):
            far = levels[np.abs(levels - a[p, g]) >= 10]
            a[p, g + 8] = far[np.random.randint(len(far))]
    return np.exp2(a.ravel()).repeat(32)


def f64(x):
    return np.asarray(x).astype(np.float64)


def striped(idx):
    return np.tile(idx.reshape(-1, 16).T, (8, 1)).astype(np.uint16)


def unstriped(offs):
    return offs[:16].T.reshape(-1).astype(np.int64)


E2M1 = np.array([0.0, 0.5, 1.0, 1.5, 2.0, 3.0, 4.0, 6.0, -0.0, -0.5, -1.0, -1.5, -2.0, -3.0, -4.0, -6.0])


def pack_weight(w, fmt):
    k, n = w.shape
    w = f64(np.asarray(w, np.float32).astype(ml_dtypes.bfloat16)).reshape(k // 32, 32, n)
    amax = np.abs(w).max(1)
    if fmt == "e4m3":
        byte = np.frexp(amax)[1] - 1 + 127 - 7
    else:
        mant, ex = np.frexp(amax / 6.0)
        byte = np.where(mant > 0.5, ex, ex - 1) + 127
    byte = np.clip(np.where(amax > 0, byte, 1), 1, 254)
    scaled = (w * np.exp2(127.0 - byte)[:, None, :]).reshape(k, n).astype(np.float32)
    by_word = np.ascontiguousarray(scaled.reshape(k // 512, 128, 4, n).transpose(0, 1, 3, 2))
    if fmt == "e4m3":
        words = by_word.astype(ml_dtypes.float8_e4m3fn).view(np.uint8)
    else:
        c = by_word.astype(ml_dtypes.float4_e2m1fn).view(np.uint8) & 0xF
        words = (c[..., 0::2] | (c[..., 1::2] << 4)).reshape(k // 512, 128, 2 * n)
    return np.ascontiguousarray(words), np.ascontiguousarray(byte.astype(np.uint8).reshape(k // 512, 16, n))


def unpack_weight(words, scales, fmt):
    g, _, n = scales.shape
    words = np.ascontiguousarray(words).reshape(g, 128, n, -1)
    if fmt == "e4m3":
        vals = words.view(ml_dtypes.float8_e4m3fn).astype(np.float64)
    else:
        nib = np.empty((g, 128, n, 4), np.uint8)
        nib[..., 0::2] = words & 0xF
        nib[..., 1::2] = words >> 4
        vals = E2M1[nib]
    vals = vals * np.repeat(np.exp2(scales.astype(np.float64) - 127.0), 8, axis=1)[..., None]
    return vals.transpose(0, 1, 3, 2).reshape(g * 512, n)


def gelu(v):
    return 0.5 * v * (1.0 + np.tanh(np.sqrt(2.0 / np.pi) * (v + 0.044715 * v**3)))


def bf(x):
    return np.asarray(x, np.float32).astype(ml_dtypes.bfloat16)

def planes(Y):
    n, m = Y.shape
    b = f64(bf(Y)).reshape(n // 32, 32, m)
    amax = np.abs(b).max(1)
    byte = np.clip(np.where(amax > 0, np.frexp(amax)[1] - 1 + 127 - 7, 1), 1, 254)
    codes = (b * np.exp2(127.0 - byte)[:, None, :]).reshape(n, m).astype(np.float32).astype(ml_dtypes.float8_e4m3fn).view(np.uint8)
    words = codes.reshape(n // 512, 128, 4, m).transpose(0, 1, 3, 2)
    return np.ascontiguousarray(words), np.ascontiguousarray(byte.astype(np.uint8).reshape(n // 512, 16, m))


K, T, S, H, N = 1024, 4096, 1024, 512, 1024

def setup_inputs():
    n = np.random.standard_normal
    s = mx_kscale(K)[:, None]
    u = mx_kscale(H)[:, None]
    cg = np.exp(0.8 * n(N))
    tab_words, tab_scales = pack_weight(n((K, T)) * s, "e4m3")
    wq_words, wq_scales = pack_weight(n((K, H)) / np.sqrt(K) / s, "e2m1")
    wg_words, wg_scales = pack_weight(0.6 * n((K, H)) / np.sqrt(K) / s, "e4m3")
    perm = np.random.permutation(T)
    return {
        "tab_words": tab_words, "tab_scales": tab_scales,
        "offs": striped(perm[:S]),
        "offs2": striped(perm[S:2 * S]),
        "offs3": striped(perm[2 * S:3 * S]),
        "wa": (n((K, H)) / np.sqrt(K) / s).astype(np.float32),
        "wq_words": wq_words, "wq_scales": wq_scales,
        "wg_words": wg_words, "wg_scales": wg_scales,
        "gain": (np.exp(0.3 * n(H)) * u[:, 0]).astype(np.float32),
        "wo": (n((H, N)) / np.sqrt(H) / u * cg).astype(np.float32),
        "bo": (0.5 * n(N) * cg).astype(np.float32),
    }

def reference(tab_words, tab_scales, offs, offs2, offs3, wa, wq_words, wq_scales, wg_words, wg_scales, gain, wo, bo):
    v1 = unpack_weight(tab_words, tab_scales, "e4m3")[:, unstriped(offs)]
    v2 = unpack_weight(tab_words, tab_scales, "e4m3")[:, unstriped(offs2)]
    v3 = unpack_weight(tab_words, tab_scales, "e4m3")[:, unstriped(offs3)]
    a = mxq(f64(wa), 0, "e4m3").T @ v1
    d = unpack_weight(wq_words, wq_scales, "e2m1").T @ v2
    c = unpack_weight(wg_words, wg_scales, "e4m3").T @ v3
    p = 1.0 / (1.0 + np.exp(-(a - d)))
    h = np.maximum(p, c) * f64(gain)[:, None]
    y = (mxq(f64(wo), 0, "e4m3").T @ mxq(h, 0, "e4m3")) + f64(bo)[:, None]
    words, scales = planes(y)
    return y, words, scales

@@ -1,0 +1,254 @@
+from contextlib import ExitStack
+
+import concourse.mybir as mybir
+
+K, T, S, H, N = 1024, 4096, 1024, 512, 1024
+FLOPS = 2 * S * H * (3 * K + N)
+
+F32 = mybir.dt.float32
+BF16 = mybir.dt.bfloat16
+I32 = mybir.dt.int32
+U32 = mybir.dt.uint32
+U16 = mybir.dt.uint16
+U8 = mybir.dt.uint8
+FP8X4 = mybir.dt.float8_e4m3fn_x4
+FP4X4 = mybir.dt.float4_e2m1fn_x4
+ACT = mybir.ActivationFunctionType
+ALU = mybir.AluOpType
+
+P = 128
+PASSES = K // 512
+GROUPS = N // 512
+HALF = 512
+CHUNK = 128
+WIDE = 256
+Y_ON_SCALAR = (1, 3, 5,)
+
+
+def tile_list_guess_floor_mastery_kernel(
+    tc, tab_words, tab_scales, offs, offs2, offs3, wa, wq_words, wq_scales, wg_words, wg_scales,
+    gain, wo, bo, out_0, out_1, out_2,
+):
+    nc = tc.nc
+    with ExitStack() as ctx:
+        keep = ctx.enter_context(tc.tile_pool(name="keep", bufs=1))
+        ring = ctx.enter_context(tc.tile_pool(name="ring", bufs=2))
+        psum = ctx.enter_context(tc.psum_pool(name="psum", bufs=1))
+
+        def held(shape, dtype, name):
+            return keep.tile(shape, dtype, name=name, align_bytes=64)
+
+        lists = [held([P, S // 16], U16, "list%d" % l) for l in range(3)]
+        tab = [held([P, T], I32, "tab%d" % a) for a in range(PASSES)]
+        tab_planes = held([P, T], U8, "tab_planes")
+        w_planes_raw = held([P, PASSES, H], U8, "w_planes_raw")
+        q_planes_1 = held([P, S], U8, "q_planes_1")
+        wa_raw = [held([P, 4, H], F32, "wa_raw%d" % a) for a in range(PASSES)]
+        wo_raw = [held([P, 4, 512], F32, "wo_raw%d" % g) for g in range(GROUPS)]
+        wq_raw = held([P, PASSES, H // 2], I32, "wq_raw")
+        wg_raw = held([P, PASSES, H], I32, "wg_raw")
+        gain_sb = held([P, 4], F32, "gain_sb")
+        gain_raw = held([P, 4, 8], F32, "gain_raw")
+        bo_sb = held([P, GROUPS, 4], F32, "bo_sb")
+        warm = held([P, 2], F32, "warm")
+
+        nc.vector.memset(tab_planes[:].bitcast(I32), 0)
+        nc.gpsimd.memset(w_planes_raw[:].rearrange("p a e -> p (a e)").bitcast(I32), 0)
+        nc.gpsimd.memset(q_planes_1[:].bitcast(I32), 0)
+        nc.gpsimd.memset(warm[:, 0:1], 0.0)
+        nc.scalar.activation(warm[:, 1:2], warm[:, 0:1], ACT.Sigmoid)
+
+        def load_tab(a):
+            nc.sync.dma_start(tab[a][:], tab_words[a].rearrange("p t i -> p (t i)").bitcast(I32))
+
+        def load_wa(a):
+            nc.sync.dma_start(wa_raw[a][:], wa[512 * a : 512 * (a + 1), :].rearrange("(p j) r -> p j r", j=4))
+
+        def load_w_planes(src, k, q):
+            nc.sync.dma_start(
+                w_planes_raw[32 * q + k : 32 * q + k + 4].bitcast(I32),
+                src[:, 4 * q : 4 * q + 4, :].rearrange("a r e -> r a e").bitcast(I32),
+            )
+
+        nc.sync.dma_start(lists[1][:], offs2)
+        for q in range(4):
+            nc.sync.dma_start(
+                tab_planes[32 * q : 32 * q + 8, :].bitcast(I32),
+                tab_scales[:, 4 * q : 4 * q + 4, :].bitcast(I32),
+            )
+        nc.sync.dma_start(lists[2][:], offs3)
+        nc.sync.dma_start(lists[0][:], offs)
+        load_tab(0)
+        load_wa(0)
+        for q in range(4):
+            load_w_planes(wg_scales, 4, q)
+        load_wa(1)
+        for q in range(4):
+            load_w_planes(wq_scales, 0, q)
+        nc.sync.dma_start(wg_raw[:], wg_words.rearrange("a p e i -> p a (e i)").bitcast(I32))
+        nc.sync.dma_start(wq_raw[:], wq_words.rearrange("a p e -> p a e").bitcast(I32))
+        load_tab(1)
+        with nc.allow_non_contiguous_dma(reason="one gain to each partition and slot"):
+            for t in range(4):
+                nc.sync.dma_start(gain_raw[:, t, 0:1], gain.rearrange("(b t q) -> t b q", t=4, q=8)[t].unsqueeze(2))
+        nc.sync.dma_start(bo_sb[:], bo.rearrange("(g p t) -> p g t", g=GROUPS, t=4))
+        wo_rows = wo.rearrange("(b t q) n -> t b q n", t=4, q=8)
+        for g in range(GROUPS):
+            for t in range(4):
+                nc.sync.dma_start(wo_raw[g][:, t, :], wo_rows[t][:, :, 512 * g : 512 * (g + 1)])
+
+        planes = [held([P, S], U8, "planes%d" % l) for l in range(3)]
+        for l in (1, 2, 0):
+            nc.vector.tensor_copy(planes[l][:], tab_planes[:].indirect(lists[l][:]))
+            if l == 1:
+                nc.scalar.dma_start(q_planes_1[0:100, :].bitcast(I32), planes[1][4:104, :].bitcast(I32))
+        words = {}
+
+        def gather(h, looks, tag):
+            room = keep.tile([P, len(looks), HALF], U32, name="room_" + tag, tag=tag, align_bytes=64)
+            cols = slice(h * HALF // 16, (h + 1) * HALF // 16)
+            for i, (l, a) in enumerate(looks):
+                words[l, a, h] = room[:, i, :]
+                nc.vector.tensor_copy(words[l, a, h], tab[a][:].bitcast(U32).indirect(lists[l][:, cols]))
+
+        for a in range(PASSES):
+            for l in (2, 1, 0):
+                gather(0, [(l, a)], "first_half%d%d" % (l, a))
+
+        wa_codes = held([P, PASSES, H], U32, "wa_codes")
+        wa_planes = held([P, PASSES, H], U8, "wa_planes")
+        for a in range(PASSES):
+            wa_bf = held([P, 4, 16, 8, 4], BF16, "wa_bf%d" % a)
+            src = wa_raw[a][:].rearrange("p j (b t q) -> p t b j q", t=4, q=8)
+            for t in range(4):
+                nc.scalar.activation(wa_bf[:, t].rearrange("p b q j -> p b j q"), src[:, t], ACT.Copy, scale=-1.0)
+            nc.vector.quantize_mx(
+                wa_codes[:, a, :].bitcast(FP8X4), wa_planes[:, a, :], wa_bf[:].rearrange("p t b q j -> p (t b q j)")
+            )
+
+        wq_codes = held([P, PASSES, 2 * H], U8, "wq_codes")
+        wg_codes = held([P, PASSES, H], I32, "wg_codes")
+        w_planes = held([P, PASSES, H], U8, "w_planes")
+        for dst, src, run in (
+            (wq_codes[:].bitcast(I32), wq_raw[:], 4),
+            (w_planes[:].bitcast(I32), w_planes_raw[:].bitcast(I32), 2),
+            (wg_codes[:], wg_raw[:], 8),
+        ):
+            nc.vector.tensor_copy(
+                dst.rearrange("p a (t b w) -> p a t b w", t=4, w=run),
+                src.rearrange("p a (b t w) -> p a t b w", t=4, w=run),
+            )
+
+
+        wo_codes = held([P, GROUPS, 512], U32, "wo_codes")
+        wo_planes = held([P, GROUPS, 512], U8, "wo_planes")
+
+        def quantize_wo(g):
+            wo_bf = held([P, 4, 128, 4], BF16, "wo_bf%d" % g)
+            nc.scalar.copy(
+                wo_bf[:].rearrange("p t m j -> p m j t"), wo_raw[g][:].rearrange("p j (m t) -> p m j t", t=4)
+            )
+            nc.vector.quantize_mx(
+                wo_codes[:, g, :].bitcast(FP8X4), wo_planes[:, g, :], wo_bf[:].rearrange("p t m j -> p (t m j)")
+            )
+
+        nc.gpsimd.tensor_copy(gain_sb[:], gain_raw[:, :, 0])
+        gather(1, [(1, 0), (0, 0)], "gain_raw")
+        y_planes = held([P, GROUPS, S], U8, "y_planes")
+        gain_bc = gain_sb[:].unsqueeze(1).to_broadcast([P, CHUNK, 4])
+        out_rows = out_0.rearrange("(g p t) j -> g p t j", g=GROUPS, t=4)
+        out_words = out_1.rearrange("g p m i -> p g (m i)").bitcast(I32)
+
+        def first_stage(c, h_bf):
+            h, u = divmod(c, HALF // CHUNK)
+            cols = slice(u * CHUNK, (u + 1) * CHUNK)
+            all_cols = slice(c * CHUNK, (c + 1) * CHUNK)
+            diff = psum.tile([P, 4, CHUNK], F32, name="diff", bufs=2)
+            guess = psum.tile([P, 4, CHUNK], F32, name="guess", bufs=3)
+            for a in range(PASSES):
+                for t in range(4):
+                    m = slice(128 * t, 128 * (t + 1))
+                    nc.tensor.matmul_mx(
+                        guess[:, t, :], lhsT=wg_codes[:, a, m].bitcast(FP8X4), lhsT_scale=w_planes[4:, a, m],
+                        rhs=words[2, a, h][:, cols].bitcast(FP8X4), rhs_scale=planes[2][4 * a :, all_cols],
+                        start=(a == 0 and t == 0), stop=(a == PASSES - 1 and t == 3),
+                    )
+            for a in range(PASSES):
+                q_plane = planes[1] if a == 0 else q_planes_1
+                for t in range(4):
+                    m = slice(128 * t, 128 * (t + 1))
+                    nc.tensor.matmul_mx(
+                        diff[:, t, :], lhsT=wq_codes[:, a, 256 * t : 256 * (t + 1)].bitcast(FP4X4),
+                        lhsT_scale=w_planes[:, a, m],
+                        rhs=words[1, a, h][:, cols].bitcast(FP8X4), rhs_scale=q_plane[:, all_cols],
+                        start=(a == 0 and t == 0), stop=False,
+                    )
+            for a in range(PASSES):
+                for t in range(4):
+                    m = slice(128 * t, 128 * (t + 1))
+                    nc.tensor.matmul_mx(
+                        diff[:, t, :], lhsT=wa_codes[:, a, m].bitcast(FP8X4), lhsT_scale=wa_planes[:, a, m],
+                        rhs=words[0, a, h][:, cols].bitcast(FP8X4), rhs_scale=planes[0][4 * a :, all_cols],
+                        start=False, stop=(a == PASSES - 1 and t == 3),
+                    )
+            success = ring.tile([P, CHUNK, 4], F32, name="success")
+            nc.scalar.activation(success[:], diff[:].rearrange("p t n -> p n t"), ACT.Sigmoid, scale=-1.0)
+            if c < 2:
+                larger = keep.tile([P, CHUNK, 4], F32, name="larger%d" % c, align_bytes=64)
+            else:
+                larger = ring.tile([P, CHUNK, 4], F32, name="larger")
+            nc.vector.tensor_tensor(larger[:], guess[:].rearrange("p t n -> p n t"), success[:], ALU.max)
+            v = c % (WIDE // CHUNK)
+            nc.vector.tensor_tensor(h_bf[:, v * CHUNK : (v + 1) * CHUNK, :], larger[:], gain_bc, ALU.mult)
+            if c == 0:
+                gather(1, [(2, 0), (2, 1)], "larger0")
+            if c == 1:
+                gather(1, [(1, 1), (0, 1)], "larger1")
+
+        def second_stage(w, h_bf):
+            cols = slice(w * WIDE, (w + 1) * WIDE)
+            h_codes = ring.tile([P, WIDE], U32, name="h_codes", align_bytes=64)
+            h_planes = ring.tile([P, WIDE], U8, name="h_planes", align_bytes=64)
+            nc.vector.quantize_mx(h_codes[:].bitcast(FP8X4), h_planes[:], h_bf[:].rearrange("p n t -> p (n t)"))
+            y_codes = held([P, GROUPS, WIDE], I32, "y_codes%d" % w)
+            for g in range(GROUPS):
+                y = held([P, 4, WIDE], F32, "y%d%d" % (w, g))
+                for pair in range(2):
+                    logits = psum.tile([P, 2, WIDE], F32, name="logits", bufs=3)
+                    for e in range(2):
+                        t = 2 * pair + e
+                        m = slice(128 * t, 128 * (t + 1))
+                        nc.tensor.matmul_mx(
+                            logits[:, e, :], lhsT=wo_codes[:, g, m].bitcast(FP8X4), lhsT_scale=wo_planes[:, g, m],
+                            rhs=h_codes[:].bitcast(FP8X4), rhs_scale=h_planes[:], start=True, stop=True,
+                        )
+                    for e in range(2):
+                        t = 2 * pair + e
+                        nc.scalar.activation(y[:, t, :], logits[:, e, :], ACT.Identity, bias=bo_sb[:, g, t : t + 1])
+                nc.sync.dma_start(out_rows[g][:, :, cols], y[:])
+                y_bf = ring.tile([P, WIDE, 4], BF16, name="y_bf", align_bytes=64, bufs=3)
+                dst = y_bf[:].rearrange("p (c i) t -> p c t i", i=4)
+                src = y[:].rearrange("p t (c i) -> p c t i", i=4)
+                if GROUPS * w + g in Y_ON_SCALAR:
+                    nc.scalar.copy(dst, src)
+                else:
+                    nc.vector.tensor_copy(dst, src)
+                nc.vector.quantize_mx(
+                    y_codes[:, g, :].bitcast(FP8X4), y_planes[:, g, cols], y_bf[:].rearrange("p n t -> p (n t)")
+                )
+            nc.sync.dma_start(out_words[:, :, cols], y_codes[:])
+
+        for w in range(S // WIDE):
+            h_bf = ring.tile([P, WIDE, 4], BF16, name="h_bf", align_bytes=64)
+            for v in range(WIDE // CHUNK):
+                first_stage(w * (WIDE // CHUNK) + v, h_bf)
+            if w == 0:
+                for g in range(GROUPS):
+                    quantize_wo(g)
+            second_stage(w, h_bf)
+
+        for q in range(4):
+            nc.sync.dma_start(
+                out_2[:, 4 * q : 4 * q + 4, :].rearrange("g r m -> r g m").bitcast(I32),
+                y_planes[32 * q : 32 * q + 4].bitcast(I32),
+            )

@@ -22,7 +22,8 @@ GROUPS = N // 512
 HALF = 512
 CHUNK = 128
 WIDE = 256
-Y_ON_SCALAR = (1, 3, 5,)
+OUT_ON_VECTOR = ()
+Y_ON_SCALAR = (0, 2,)
 
 
 def tile_list_guess_floor_mastery_kernel(
@@ -70,14 +71,23 @@ def tile_list_guess_floor_mastery_kernel(
                 src[:, 4 * q : 4 * q + 4, :].rearrange("a r e -> r a e").bitcast(I32),
             )
 
-        nc.sync.dma_start(lists[1][:], offs2)
+        wo_rows = wo.rearrange("(b t q) n -> t b q n", t=4, q=8)
+
+        def load_wo(g):
+            for t in range(4):
+                nc.sync.dma_start(wo_raw[g][:, t, :], wo_rows[t][:, :, 512 * g : 512 * (g + 1)])
+
         for q in range(4):
             nc.sync.dma_start(
                 tab_planes[32 * q : 32 * q + 8, :].bitcast(I32),
                 tab_scales[:, 4 * q : 4 * q + 4, :].bitcast(I32),
             )
-        nc.sync.dma_start(lists[2][:], offs3)
-        nc.sync.dma_start(lists[0][:], offs)
+        for l, src in ((1, offs2), (2, offs3), (0, offs)):
+            nc.sync.dma_start(lists[l][:], src)
+        with nc.allow_non_contiguous_dma(reason="one gain to each partition and slot"):
+            for t in range(4):
+                nc.sync.dma_start(gain_raw[:, t, 0:1], gain.rearrange("(b t q) -> t b q", t=4, q=8)[t].unsqueeze(2))
+        nc.sync.dma_start(bo_sb[:], bo.rearrange("(g p t) -> p g t", g=GROUPS, t=4))
         load_tab(0)
         load_wa(0)
         for q in range(4):
@@ -86,16 +96,10 @@ def tile_list_guess_floor_mastery_kernel(
         for q in range(4):
             load_w_planes(wq_scales, 0, q)
         nc.sync.dma_start(wg_raw[:], wg_words.rearrange("a p e i -> p a (e i)").bitcast(I32))
-        nc.sync.dma_start(wq_raw[:], wq_words.rearrange("a p e -> p a e").bitcast(I32))
+        load_wo(0)
         load_tab(1)
-        with nc.allow_non_contiguous_dma(reason="one gain to each partition and slot"):
-            for t in range(4):
-                nc.sync.dma_start(gain_raw[:, t, 0:1], gain.rearrange("(b t q) -> t b q", t=4, q=8)[t].unsqueeze(2))
-        nc.sync.dma_start(bo_sb[:], bo.rearrange("(g p t) -> p g t", g=GROUPS, t=4))
-        wo_rows = wo.rearrange("(b t q) n -> t b q n", t=4, q=8)
-        for g in range(GROUPS):
-            for t in range(4):
-                nc.sync.dma_start(wo_raw[g][:, t, :], wo_rows[t][:, :, 512 * g : 512 * (g + 1)])
+        nc.sync.dma_start(wq_raw[:], wq_words.rearrange("a p e -> p a e").bitcast(I32))
+        load_wo(1)
 
         planes = [held([P, S], U8, "planes%d" % l) for l in range(3)]
         for l in (1, 2, 0):
@@ -111,17 +115,17 @@ def tile_list_guess_floor_mastery_kernel(
                 words[l, a, h] = room[:, i, :]
                 nc.vector.tensor_copy(words[l, a, h], tab[a][:].bitcast(U32).indirect(lists[l][:, cols]))
 
-        for a in range(PASSES):
-            for l in (2, 1, 0):
-                gather(0, [(l, a)], "first_half%d%d" % (l, a))
+        for a, h in ((0, 0), (0, 1), (1, 0)):
+            for l in (2, 0, 1):
+                gather(h, [(l, a)], "early%d%d%d" % (l, a, h))
 
         wa_codes = held([P, PASSES, H], U32, "wa_codes")
         wa_planes = held([P, PASSES, H], U8, "wa_planes")
         for a in range(PASSES):
             wa_bf = held([P, 4, 16, 8, 4], BF16, "wa_bf%d" % a)
-            src = wa_raw[a][:].rearrange("p j (b t q) -> p t b j q", t=4, q=8)
+            src = wa_raw[a][:].rearrange("p j (b t q) -> p t b q j", t=4, q=8)
             for t in range(4):
-                nc.scalar.activation(wa_bf[:, t].rearrange("p b q j -> p b j q"), src[:, t], ACT.Copy, scale=-1.0)
+                nc.scalar.activation(wa_bf[:, t], src[:, t], ACT.Copy, scale=-1.0)
             nc.vector.quantize_mx(
                 wa_codes[:, a, :].bitcast(FP8X4), wa_planes[:, a, :], wa_bf[:].rearrange("p t b q j -> p (t b q j)")
             )
@@ -130,9 +134,9 @@ def tile_list_guess_floor_mastery_kernel(
         wg_codes = held([P, PASSES, H], I32, "wg_codes")
         w_planes = held([P, PASSES, H], U8, "w_planes")
         for dst, src, run in (
-            (wq_codes[:].bitcast(I32), wq_raw[:], 4),
             (w_planes[:].bitcast(I32), w_planes_raw[:].bitcast(I32), 2),
             (wg_codes[:], wg_raw[:], 8),
+            (wq_codes[:].bitcast(I32), wq_raw[:], 4),
         ):
             nc.vector.tensor_copy(
                 dst.rearrange("p a (t b w) -> p a t b w", t=4, w=run),
@@ -145,15 +149,17 @@ def tile_list_guess_floor_mastery_kernel(
 
         def quantize_wo(g):
             wo_bf = held([P, 4, 128, 4], BF16, "wo_bf%d" % g)
-            nc.scalar.copy(
-                wo_bf[:].rearrange("p t m j -> p m j t"), wo_raw[g][:].rearrange("p j (m t) -> p m j t", t=4)
-            )
+            dst = wo_bf[:].rearrange("p t m j -> p m t j")
+            src = wo_raw[g][:].rearrange("p j (m t) -> p m t j", t=4)
+            for m in range(0, 128, 32):
+                nc.scalar.copy(dst[:, m : m + 32], src[:, m : m + 32])
             nc.vector.quantize_mx(
                 wo_codes[:, g, :].bitcast(FP8X4), wo_planes[:, g, :], wo_bf[:].rearrange("p t m j -> p (t m j)")
             )
 
+        quantize_wo(0)
         nc.gpsimd.tensor_copy(gain_sb[:], gain_raw[:, :, 0])
-        gather(1, [(1, 0), (0, 0)], "gain_raw")
+        gather(1, [(2, 1)], "wq_raw")
         y_planes = held([P, GROUPS, S], U8, "y_planes")
         gain_bc = gain_sb[:].unsqueeze(1).to_broadcast([P, CHUNK, 4])
         out_rows = out_0.rearrange("(g p t) j -> g p t j", g=GROUPS, t=4)
@@ -174,6 +180,14 @@ def tile_list_guess_floor_mastery_kernel(
                         start=(a == 0 and t == 0), stop=(a == PASSES - 1 and t == 3),
                     )
             for a in range(PASSES):
+                for t in range(4):
+                    m = slice(128 * t, 128 * (t + 1))
+                    nc.tensor.matmul_mx(
+                        diff[:, t, :], lhsT=wa_codes[:, a, m].bitcast(FP8X4), lhsT_scale=wa_planes[:, a, m],
+                        rhs=words[0, a, h][:, cols].bitcast(FP8X4), rhs_scale=planes[0][4 * a :, all_cols],
+                        start=(a == 0 and t == 0), stop=False,
+                    )
+            for a in range(PASSES):
                 q_plane = planes[1] if a == 0 else q_planes_1
                 for t in range(4):
                     m = slice(128 * t, 128 * (t + 1))
@@ -181,38 +195,32 @@ def tile_list_guess_floor_mastery_kernel(
                         diff[:, t, :], lhsT=wq_codes[:, a, 256 * t : 256 * (t + 1)].bitcast(FP4X4),
                         lhsT_scale=w_planes[:, a, m],
                         rhs=words[1, a, h][:, cols].bitcast(FP8X4), rhs_scale=q_plane[:, all_cols],
-                        start=(a == 0 and t == 0), stop=False,
-                    )
-            for a in range(PASSES):
-                for t in range(4):
-                    m = slice(128 * t, 128 * (t + 1))
-                    nc.tensor.matmul_mx(
-                        diff[:, t, :], lhsT=wa_codes[:, a, m].bitcast(FP8X4), lhsT_scale=wa_planes[:, a, m],
-                        rhs=words[0, a, h][:, cols].bitcast(FP8X4), rhs_scale=planes[0][4 * a :, all_cols],
                         start=False, stop=(a == PASSES - 1 and t == 3),
                     )
-            success = ring.tile([P, CHUNK, 4], F32, name="success")
+            success = ring.tile([P, CHUNK, 4], F32, name="success", bufs=3)
             nc.scalar.activation(success[:], diff[:].rearrange("p t n -> p n t"), ACT.Sigmoid, scale=-1.0)
-            if c < 2:
+            if c < 4:
                 larger = keep.tile([P, CHUNK, 4], F32, name="larger%d" % c, align_bytes=64)
             else:
                 larger = ring.tile([P, CHUNK, 4], F32, name="larger")
             nc.vector.tensor_tensor(larger[:], guess[:].rearrange("p t n -> p n t"), success[:], ALU.max)
             v = c % (WIDE // CHUNK)
             nc.vector.tensor_tensor(h_bf[:, v * CHUNK : (v + 1) * CHUNK, :], larger[:], gain_bc, ALU.mult)
-            if c == 0:
-                gather(1, [(2, 0), (2, 1)], "larger0")
-            if c == 1:
-                gather(1, [(1, 1), (0, 1)], "larger1")
 
-        def second_stage(w, h_bf):
-            cols = slice(w * WIDE, (w + 1) * WIDE)
-            h_codes = ring.tile([P, WIDE], U32, name="h_codes", align_bytes=64)
-            h_planes = ring.tile([P, WIDE], U8, name="h_planes", align_bytes=64)
+        h_mx, ys = {}, {}
+
+        def quantize_h(w, h_bf):
+            h_codes = ring.tile([P, WIDE], U32, name="h_codes", align_bytes=64, bufs=3)
+            h_planes = ring.tile([P, WIDE], U8, name="h_planes", align_bytes=64, bufs=3)
             nc.vector.quantize_mx(h_codes[:].bitcast(FP8X4), h_planes[:], h_bf[:].rearrange("p n t -> p (n t)"))
-            y_codes = held([P, GROUPS, WIDE], I32, "y_codes%d" % w)
+            h_mx[w] = (h_codes, h_planes)
+
+        def second_stage(w):
+            cols = slice(w * WIDE, (w + 1) * WIDE)
+            h_codes, h_planes = h_mx[w]
             for g in range(GROUPS):
                 y = held([P, 4, WIDE], F32, "y%d%d" % (w, g))
+                ys[w, g] = y
                 for pair in range(2):
                     logits = psum.tile([P, 2, WIDE], F32, name="logits", bufs=3)
                     for e in range(2):
@@ -224,11 +232,19 @@ def tile_list_guess_floor_mastery_kernel(
                         )
                     for e in range(2):
                         t = 2 * pair + e
-                        nc.scalar.activation(y[:, t, :], logits[:, e, :], ACT.Identity, bias=bo_sb[:, g, t : t + 1])
+                        if (w, g, pair) in OUT_ON_VECTOR:
+                            nc.vector.tensor_scalar(y[:, t, :], logits[:, e, :], bo_sb[:, g, t : t + 1], None, ALU.add)
+                        else:
+                            nc.scalar.activation(y[:, t, :], logits[:, e, :], ACT.Identity, bias=bo_sb[:, g, t : t + 1])
                 nc.sync.dma_start(out_rows[g][:, :, cols], y[:])
+
+        def result_planes(w):
+            cols = slice(w * WIDE, (w + 1) * WIDE)
+            y_codes = held([P, GROUPS, WIDE], I32, "y_codes%d" % w)
+            for g in range(GROUPS):
                 y_bf = ring.tile([P, WIDE, 4], BF16, name="y_bf", align_bytes=64, bufs=3)
                 dst = y_bf[:].rearrange("p (c i) t -> p c t i", i=4)
-                src = y[:].rearrange("p t (c i) -> p c t i", i=4)
+                src = ys[w, g][:].rearrange("p t (c i) -> p c t i", i=4)
                 if GROUPS * w + g in Y_ON_SCALAR:
                     nc.scalar.copy(dst, src)
                 else:
@@ -238,14 +254,23 @@ def tile_list_guess_floor_mastery_kernel(
                 )
             nc.sync.dma_start(out_words[:, :, cols], y_codes[:])
 
-        for w in range(S // WIDE):
-            h_bf = ring.tile([P, WIDE, 4], BF16, name="h_bf", align_bytes=64)
-            for v in range(WIDE // CHUNK):
-                first_stage(w * (WIDE // CHUNK) + v, h_bf)
+        wides = S // WIDE
+        for w in range(wides + 2):
+            if w < wides:
+                h_bf = held([P, WIDE, 4], BF16, "h_bf%d" % w)
+                for v in range(WIDE // CHUNK):
+                    first_stage(w * (WIDE // CHUNK) + v, h_bf)
+                quantize_h(w, h_bf)
             if w == 0:
-                for g in range(GROUPS):
-                    quantize_wo(g)
-            second_stage(w, h_bf)
+                quantize_wo(1)
+            if w == 0:
+                gather(1, [(0, 1)], "larger0")
+            if w == 0:
+                gather(1, [(1, 1)], "larger1")
+            if 0 <= w - 1 < wides:
+                second_stage(w - 1)
+            if 0 <= w - 2 < wides:
+                result_planes(w - 2)
 
         for q in range(4):
             nc.sync.dma_start(

@@ -21,9 +21,10 @@ PASSES = K // 512
 GROUPS = N // 512
 HALF = 512
 CHUNK = 128
-WIDE = 256
+STRIPS = (2, 2, 2, 2)
+FIRST = [sum(STRIPS[:w]) for w in range(len(STRIPS))]
 OUT_ON_VECTOR = ()
-Y_ON_SCALAR = (0, 2,)
+Y_ON_SCALAR = (0, 2, 4,)
 
 
 def tile_list_guess_floor_mastery_kernel(
@@ -48,15 +49,15 @@ def tile_list_guess_floor_mastery_kernel(
         wo_raw = [held([P, 4, 512], F32, "wo_raw%d" % g) for g in range(GROUPS)]
         wq_raw = held([P, PASSES, H // 2], I32, "wq_raw")
         wg_raw = held([P, PASSES, H], I32, "wg_raw")
-        gain_sb = held([P, 4], F32, "gain_sb")
+        gain_sb = held([P, CHUNK, 4], F32, "gain_sb")
         gain_raw = held([P, 4, 8], F32, "gain_raw")
         bo_sb = held([P, GROUPS, 4], F32, "bo_sb")
         warm = held([P, 2], F32, "warm")
 
         nc.vector.memset(tab_planes[:].bitcast(I32), 0)
-        nc.gpsimd.memset(w_planes_raw[:].rearrange("p a e -> p (a e)").bitcast(I32), 0)
-        nc.gpsimd.memset(q_planes_1[:].bitcast(I32), 0)
-        nc.gpsimd.memset(warm[:, 0:1], 0.0)
+        nc.vector.memset(w_planes_raw[:].rearrange("p a e -> p (a e)").bitcast(I32), 0)
+        nc.vector.memset(q_planes_1[:].bitcast(I32), 0)
+        nc.vector.memset(warm[:, 0:1], 0.0)
         nc.scalar.activation(warm[:, 1:2], warm[:, 0:1], ACT.Sigmoid)
 
         def load_tab(a):
@@ -77,17 +78,15 @@ def tile_list_guess_floor_mastery_kernel(
             for t in range(4):
                 nc.sync.dma_start(wo_raw[g][:, t, :], wo_rows[t][:, :, 512 * g : 512 * (g + 1)])
 
+        nc.sync.dma_start(lists[1][:], offs2)
         for q in range(4):
-            nc.sync.dma_start(
-                tab_planes[32 * q : 32 * q + 8, :].bitcast(I32),
-                tab_scales[:, 4 * q : 4 * q + 4, :].bitcast(I32),
-            )
-        for l, src in ((1, offs2), (2, offs3), (0, offs)):
+            for a in range(PASSES):
+                nc.sync.dma_start(
+                    tab_planes[32 * q + 4 * a : 32 * q + 4 * a + 4, :].bitcast(I32),
+                    tab_scales[a, 4 * q : 4 * q + 4, :].bitcast(I32),
+                )
+        for l, src in ((2, offs3), (0, offs)):
             nc.sync.dma_start(lists[l][:], src)
-        with nc.allow_non_contiguous_dma(reason="one gain to each partition and slot"):
-            for t in range(4):
-                nc.sync.dma_start(gain_raw[:, t, 0:1], gain.rearrange("(b t q) -> t b q", t=4, q=8)[t].unsqueeze(2))
-        nc.sync.dma_start(bo_sb[:], bo.rearrange("(g p t) -> p g t", g=GROUPS, t=4))
         load_tab(0)
         load_wa(0)
         for q in range(4):
@@ -96,16 +95,20 @@ def tile_list_guess_floor_mastery_kernel(
         for q in range(4):
             load_w_planes(wq_scales, 0, q)
         nc.sync.dma_start(wg_raw[:], wg_words.rearrange("a p e i -> p a (e i)").bitcast(I32))
-        load_wo(0)
         load_tab(1)
         nc.sync.dma_start(wq_raw[:], wq_words.rearrange("a p e -> p a e").bitcast(I32))
+        with nc.allow_non_contiguous_dma(reason="one gain to each partition and slot"):
+            for t in range(4):
+                nc.sync.dma_start(gain_raw[:, t, 0:1], gain.rearrange("(b t q) -> t b q", t=4, q=8)[t].unsqueeze(2))
+        nc.sync.dma_start(bo_sb[:], bo.rearrange("(g p t) -> p g t", g=GROUPS, t=4))
+        load_wo(0)
         load_wo(1)
 
         planes = [held([P, S], U8, "planes%d" % l) for l in range(3)]
         for l in (1, 2, 0):
             nc.vector.tensor_copy(planes[l][:], tab_planes[:].indirect(lists[l][:]))
             if l == 1:
-                nc.scalar.dma_start(q_planes_1[0:100, :].bitcast(I32), planes[1][4:104, :].bitcast(I32))
+                nc.sync.dma_start(q_planes_1[0:100, :].bitcast(I32), planes[1][4:104, :].bitcast(I32))
         words = {}
 
         def gather(h, looks, tag):
@@ -115,9 +118,8 @@ def tile_list_guess_floor_mastery_kernel(
                 words[l, a, h] = room[:, i, :]
                 nc.vector.tensor_copy(words[l, a, h], tab[a][:].bitcast(U32).indirect(lists[l][:, cols]))
 
-        for a, h in ((0, 0), (0, 1), (1, 0)):
-            for l in (2, 0, 1):
-                gather(h, [(l, a)], "early%d%d%d" % (l, a, h))
+        for l, a, h in ((2, 0, 0), (0, 0, 0), (1, 0, 0), (2, 0, 1), (0, 0, 1), (2, 1, 0), (0, 1, 0), (1, 1, 0)):
+            gather(h, [(l, a)], "early%d%d%d" % (l, a, h))
 
         wa_codes = held([P, PASSES, H], U32, "wa_codes")
         wa_planes = held([P, PASSES, H], U8, "wa_planes")
@@ -158,14 +160,14 @@ def tile_list_guess_floor_mastery_kernel(
             )
 
         quantize_wo(0)
-        nc.gpsimd.tensor_copy(gain_sb[:], gain_raw[:, :, 0])
-        gather(1, [(2, 1)], "wq_raw")
+        nc.scalar.copy(gain_sb[:], gain_raw[:, :, 0].unsqueeze(1).to_broadcast([P, CHUNK, 4]))
+        gather(1, [(2, 1), (1, 0)], "wq_raw")
         y_planes = held([P, GROUPS, S], U8, "y_planes")
-        gain_bc = gain_sb[:].unsqueeze(1).to_broadcast([P, CHUNK, 4])
+        gain_bc = gain_sb[:]
         out_rows = out_0.rearrange("(g p t) j -> g p t j", g=GROUPS, t=4)
         out_words = out_1.rearrange("g p m i -> p g (m i)").bitcast(I32)
 
-        def first_stage(c, h_bf):
+        def first_stage(c, h_bf, v):
             h, u = divmod(c, HALF // CHUNK)
             cols = slice(u * CHUNK, (u + 1) * CHUNK)
             all_cols = slice(c * CHUNK, (c + 1) * CHUNK)
@@ -204,34 +206,36 @@ def tile_list_guess_floor_mastery_kernel(
             else:
                 larger = ring.tile([P, CHUNK, 4], F32, name="larger")
             nc.vector.tensor_tensor(larger[:], guess[:].rearrange("p t n -> p n t"), success[:], ALU.max)
-            v = c % (WIDE // CHUNK)
             nc.vector.tensor_tensor(h_bf[:, v * CHUNK : (v + 1) * CHUNK, :], larger[:], gain_bc, ALU.mult)
 
         h_mx, ys = {}, {}
 
         def quantize_h(w, h_bf):
-            h_codes = ring.tile([P, WIDE], U32, name="h_codes", align_bytes=64, bufs=3)
-            h_planes = ring.tile([P, WIDE], U8, name="h_planes", align_bytes=64, bufs=3)
+            width = STRIPS[w] * CHUNK
+            h_codes = ring.tile([P, width], U32, name="h_codes", align_bytes=64, bufs=3)
+            h_planes = ring.tile([P, width], U8, name="h_planes", align_bytes=64, bufs=3)
             nc.vector.quantize_mx(h_codes[:].bitcast(FP8X4), h_planes[:], h_bf[:].rearrange("p n t -> p (n t)"))
             h_mx[w] = (h_codes, h_planes)
 
         def second_stage(w):
-            cols = slice(w * WIDE, (w + 1) * WIDE)
+            width = STRIPS[w] * CHUNK
+            cols = slice(FIRST[w] * CHUNK, FIRST[w] * CHUNK + width)
             h_codes, h_planes = h_mx[w]
             for g in range(GROUPS):
-                y = held([P, 4, WIDE], F32, "y%d%d" % (w, g))
+                y = held([P, 4, width], F32, "y%d%d" % (w, g))
                 ys[w, g] = y
-                for pair in range(2):
-                    logits = psum.tile([P, 2, WIDE], F32, name="logits", bufs=3)
-                    for e in range(2):
-                        t = 2 * pair + e
+                per_bank = 512 // width
+                for pair in range(4 // per_bank):
+                    logits = psum.tile([P, per_bank, width], F32, name="logits", bufs=3)
+                    for e in range(per_bank):
+                        t = per_bank * pair + e
                         m = slice(128 * t, 128 * (t + 1))
                         nc.tensor.matmul_mx(
                             logits[:, e, :], lhsT=wo_codes[:, g, m].bitcast(FP8X4), lhsT_scale=wo_planes[:, g, m],
                             rhs=h_codes[:].bitcast(FP8X4), rhs_scale=h_planes[:], start=True, stop=True,
                         )
-                    for e in range(2):
-                        t = 2 * pair + e
+                    for e in range(per_bank):
+                        t = per_bank * pair + e
                         if (w, g, pair) in OUT_ON_VECTOR:
                             nc.vector.tensor_scalar(y[:, t, :], logits[:, e, :], bo_sb[:, g, t : t + 1], None, ALU.add)
                         else:
@@ -239,12 +243,13 @@ def tile_list_guess_floor_mastery_kernel(
                 nc.sync.dma_start(out_rows[g][:, :, cols], y[:])
 
         def result_planes(w):
-            cols = slice(w * WIDE, (w + 1) * WIDE)
-            y_codes = held([P, GROUPS, WIDE], I32, "y_codes%d" % w)
+            width = STRIPS[w] * CHUNK
+            cols = slice(FIRST[w] * CHUNK, FIRST[w] * CHUNK + width)
+            y_codes = held([P, GROUPS, width], I32, "y_codes%d" % w)
             for g in range(GROUPS):
-                y_bf = ring.tile([P, WIDE, 4], BF16, name="y_bf", align_bytes=64, bufs=3)
-                dst = y_bf[:].rearrange("p (c i) t -> p c t i", i=4)
-                src = ys[w, g][:].rearrange("p t (c i) -> p c t i", i=4)
+                y_bf = ring.tile([P, width, 4], BF16, name="y_bf", align_bytes=64, bufs=3)
+                dst = y_bf[:]
+                src = ys[w, g][:].rearrange("p t n -> p n t")
                 if GROUPS * w + g in Y_ON_SCALAR:
                     nc.scalar.copy(dst, src)
                 else:
@@ -254,19 +259,19 @@ def tile_list_guess_floor_mastery_kernel(
                 )
             nc.sync.dma_start(out_words[:, :, cols], y_codes[:])
 
-        wides = S // WIDE
+        wides = len(STRIPS)
         for w in range(wides + 2):
             if w < wides:
-                h_bf = held([P, WIDE, 4], BF16, "h_bf%d" % w)
-                for v in range(WIDE // CHUNK):
-                    first_stage(w * (WIDE // CHUNK) + v, h_bf)
+                h_bf = held([P, STRIPS[w] * CHUNK, 4], BF16, "h_bf%d" % w)
+                for v in range(STRIPS[w]):
+                    first_stage(FIRST[w] + v, h_bf, v)
                 quantize_h(w, h_bf)
-            if w == 0:
-                quantize_wo(1)
             if w == 0:
                 gather(1, [(0, 1)], "larger0")
             if w == 0:
                 gather(1, [(1, 1)], "larger1")
+            if w == 0:
+                quantize_wo(1)
             if 0 <= w - 1 < wides:
                 second_stage(w - 1)
             if 0 <= w - 2 < wides:

@@ -20,11 +20,13 @@ P = 128
 PASSES = K // 512
 GROUPS = N // 512
 HALF = 512
+ROW0 = 96
 CHUNK = 128
-STRIPS = (2, 2, 2, 2)
+STRIPS = (2, 2, 2, 2,)
 FIRST = [sum(STRIPS[:w]) for w in range(len(STRIPS))]
 OUT_ON_VECTOR = ()
 Y_ON_SCALAR = (0, 2, 4,)
+WHOLE_GAIN = ()
 
 
 def tile_list_guess_floor_mastery_kernel(
@@ -37,27 +39,27 @@ def tile_list_guess_floor_mastery_kernel(
         ring = ctx.enter_context(tc.tile_pool(name="ring", bufs=2))
         psum = ctx.enter_context(tc.psum_pool(name="psum", bufs=1))
 
-        def held(shape, dtype, name):
-            return keep.tile(shape, dtype, name=name, align_bytes=64)
+        def held(shape, dtype, name, tag=None):
+            return keep.tile(shape, dtype, name=name, tag=tag or name, align_bytes=64)
 
         lists = [held([P, S // 16], U16, "list%d" % l) for l in range(3)]
         tab = [held([P, T], I32, "tab%d" % a) for a in range(PASSES)]
-        tab_planes = held([P, T], U8, "tab_planes")
-        w_planes_raw = held([P, PASSES, H], U8, "w_planes_raw")
-        q_planes_1 = held([P, S], U8, "q_planes_1")
+        tab_rows = held([P, T], U8, "tab_rows")
+        w_rows = held([P, 2, H], U8, "w_rows")
+        staged = held([P, 3 * S + 2 * H], U8, "staged")
+        planes = held([P, PASSES, 3 * S + 2 * H], U8, "planes")
         wa_raw = [held([P, 4, H], F32, "wa_raw%d" % a) for a in range(PASSES)]
-        wo_raw = [held([P, 4, 512], F32, "wo_raw%d" % g) for g in range(GROUPS)]
+        picked = held([P, 3, S], U8, "picked")
         wq_raw = held([P, PASSES, H // 2], I32, "wq_raw")
         wg_raw = held([P, PASSES, H], I32, "wg_raw")
-        gain_sb = held([P, CHUNK, 4], F32, "gain_sb")
+        gain_sb = held([P, CHUNK * 4], F32, "gain_sb")
         gain_raw = held([P, 4, 8], F32, "gain_raw")
         bo_sb = held([P, GROUPS, 4], F32, "bo_sb")
         warm = held([P, 2], F32, "warm")
 
-        nc.vector.memset(tab_planes[:].bitcast(I32), 0)
-        nc.vector.memset(w_planes_raw[:].rearrange("p a e -> p (a e)").bitcast(I32), 0)
-        nc.vector.memset(q_planes_1[:].bitcast(I32), 0)
+        nc.vector.memset(tab_rows[0:ROW0, :].bitcast(I32), 0)
         nc.vector.memset(warm[:, 0:1], 0.0)
+        nc.vector.memset(planes[:].rearrange("p a e -> p (a e)").bitcast(I32), 0)
         nc.scalar.activation(warm[:, 1:2], warm[:, 0:1], ACT.Sigmoid)
 
         def load_tab(a):
@@ -66,60 +68,60 @@ def tile_list_guess_floor_mastery_kernel(
         def load_wa(a):
             nc.sync.dma_start(wa_raw[a][:], wa[512 * a : 512 * (a + 1), :].rearrange("(p j) r -> p j r", j=4))
 
-        def load_w_planes(src, k, q):
-            nc.sync.dma_start(
-                w_planes_raw[32 * q + k : 32 * q + k + 4].bitcast(I32),
-                src[:, 4 * q : 4 * q + 4, :].rearrange("a r e -> r a e").bitcast(I32),
-            )
+        def load_gain(t):
+            with nc.allow_non_contiguous_dma(reason="one gain to each partition and slot"):
+                nc.sync.dma_start(gain_raw[:, t, 0:1], gain.rearrange("(b t q) -> t b q", t=4, q=8)[t].unsqueeze(2))
 
         wo_rows = wo.rearrange("(b t q) n -> t b q n", t=4, q=8)
+        wo_raw = {}
 
-        def load_wo(g):
+        def load_wo(g, tag):
+            wo_raw[g] = held([P, 4, 512], F32, "wo_raw%d" % g, tag)
             for t in range(4):
                 nc.sync.dma_start(wo_raw[g][:, t, :], wo_rows[t][:, :, 512 * g : 512 * (g + 1)])
 
-        nc.sync.dma_start(lists[1][:], offs2)
-        for q in range(4):
-            for a in range(PASSES):
-                nc.sync.dma_start(
-                    tab_planes[32 * q + 4 * a : 32 * q + 4 * a + 4, :].bitcast(I32),
-                    tab_scales[a, 4 * q : 4 * q + 4, :].bitcast(I32),
-                )
-        for l, src in ((2, offs3), (0, offs)):
+        nc.sync.dma_start(tab_rows[ROW0:, :].bitcast(I32), tab_scales.rearrange("a q t -> (a q) t").bitcast(I32))
+        for l, src in enumerate((offs, offs2, offs3)):
             nc.sync.dma_start(lists[l][:], src)
-        load_tab(0)
+        for i, src in enumerate((wq_scales, wg_scales)):
+            nc.sync.dma_start(w_rows[ROW0:, i, :].bitcast(I32), src.rearrange("a q e -> (a q) e").bitcast(I32))
         load_wa(0)
-        for q in range(4):
-            load_w_planes(wg_scales, 4, q)
+        load_tab(0)
+        load_gain(0)
+        load_gain(1)
         load_wa(1)
-        for q in range(4):
-            load_w_planes(wq_scales, 0, q)
+        load_gain(2)
+        load_gain(3)
+        nc.sync.dma_start(wq_raw[:], wq_words.rearrange("a p e -> p a e").bitcast(I32))
         nc.sync.dma_start(wg_raw[:], wg_words.rearrange("a p e i -> p a (e i)").bitcast(I32))
         load_tab(1)
-        nc.sync.dma_start(wq_raw[:], wq_words.rearrange("a p e -> p a e").bitcast(I32))
-        with nc.allow_non_contiguous_dma(reason="one gain to each partition and slot"):
-            for t in range(4):
-                nc.sync.dma_start(gain_raw[:, t, 0:1], gain.rearrange("(b t q) -> t b q", t=4, q=8)[t].unsqueeze(2))
         nc.sync.dma_start(bo_sb[:], bo.rearrange("(g p t) -> p g t", g=GROUPS, t=4))
-        load_wo(0)
-        load_wo(1)
 
-        planes = [held([P, S], U8, "planes%d" % l) for l in range(3)]
-        for l in (1, 2, 0):
-            nc.vector.tensor_copy(planes[l][:], tab_planes[:].indirect(lists[l][:]))
-            if l == 1:
-                nc.sync.dma_start(q_planes_1[0:100, :].bitcast(I32), planes[1][4:104, :].bitcast(I32))
+        for l in range(3):
+            nc.vector.tensor_copy(picked[:, l, :], tab_rows[:].indirect(lists[l][:]))
+        nc.vector.tensor_copy(
+            staged[ROW0:, 3 * S :].bitcast(I32).rearrange("p (i t b w) -> p i t b w", i=2, t=4, w=2),
+            w_rows[ROW0:].bitcast(I32).rearrange("p i (b t w) -> p i t b w", t=4, w=2),
+        )
+        nc.vector.tensor_copy(
+            staged[ROW0:, : 3 * S].bitcast(I32), picked[ROW0:].rearrange("p l s -> p (l s)").bitcast(I32)
+        )
+        for a in range(PASSES):
+            for q in range(4):
+                row = ROW0 + 16 * a + 4 * q
+                nc.sync.dma_start(planes[32 * q : 32 * q + 4, a, :].bitcast(I32), staged[row : row + 4, :].bitcast(I32))
+        load_wo(0, "picked")
         words = {}
 
-        def gather(h, looks, tag):
-            room = keep.tile([P, len(looks), HALF], U32, name="room_" + tag, tag=tag, align_bytes=64)
-            cols = slice(h * HALF // 16, (h + 1) * HALF // 16)
-            for i, (l, a) in enumerate(looks):
-                words[l, a, h] = room[:, i, :]
-                nc.vector.tensor_copy(words[l, a, h], tab[a][:].bitcast(U32).indirect(lists[l][:, cols]))
+        def gather(l, a, first, count, tag):
+            room = held([P, count * HALF], U32, "room%d%d%d" % (l, a, first), tag)
+            cols = slice(first * HALF // 16, (first + count) * HALF // 16)
+            nc.vector.tensor_copy(room[:], tab[a][:].bitcast(U32).indirect(lists[l][:, cols]))
+            for i in range(count):
+                words[l, a, first + i] = room[:, i * HALF : (i + 1) * HALF]
 
-        for l, a, h in ((2, 0, 0), (0, 0, 0), (1, 0, 0), (2, 0, 1), (0, 0, 1), (2, 1, 0), (0, 1, 0), (1, 1, 0)):
-            gather(h, [(l, a)], "early%d%d%d" % (l, a, h))
+        for l in range(3):
+            gather(l, 0, 0, 2, None)
 
         wa_codes = held([P, PASSES, H], U32, "wa_codes")
         wa_planes = held([P, PASSES, H], U8, "wa_planes")
@@ -134,23 +136,23 @@ def tile_list_guess_floor_mastery_kernel(
 
         wq_codes = held([P, PASSES, 2 * H], U8, "wq_codes")
         wg_codes = held([P, PASSES, H], I32, "wg_codes")
-        w_planes = held([P, PASSES, H], U8, "w_planes")
+        load_wo(1, "wa_raw1")
         for dst, src, run in (
-            (w_planes[:].bitcast(I32), w_planes_raw[:].bitcast(I32), 2),
-            (wg_codes[:], wg_raw[:], 8),
             (wq_codes[:].bitcast(I32), wq_raw[:], 4),
+            (wg_codes[:], wg_raw[:], 8),
         ):
             nc.vector.tensor_copy(
                 dst.rearrange("p a (t b w) -> p a t b w", t=4, w=run),
                 src.rearrange("p a (b t w) -> p a t b w", t=4, w=run),
             )
-
+        for l in range(3):
+            gather(l, 1, 0, 1, None)
 
         wo_codes = held([P, GROUPS, 512], U32, "wo_codes")
         wo_planes = held([P, GROUPS, 512], U8, "wo_planes")
 
         def quantize_wo(g):
-            wo_bf = held([P, 4, 128, 4], BF16, "wo_bf%d" % g)
+            wo_bf = held([P, 4, 128, 4], BF16, "wo_bf%d" % g, "wa_bf%d" % g)
             dst = wo_bf[:].rearrange("p t m j -> p m t j")
             src = wo_raw[g][:].rearrange("p j (m t) -> p m t j", t=4)
             for m in range(0, 128, 32):
@@ -159,54 +161,54 @@ def tile_list_guess_floor_mastery_kernel(
                 wo_codes[:, g, :].bitcast(FP8X4), wo_planes[:, g, :], wo_bf[:].rearrange("p t m j -> p (t m j)")
             )
 
-        quantize_wo(0)
-        nc.scalar.copy(gain_sb[:], gain_raw[:, :, 0].unsqueeze(1).to_broadcast([P, CHUNK, 4]))
-        gather(1, [(2, 1), (1, 0)], "wq_raw")
+        nc.scalar.copy(
+            gain_sb[:].rearrange("p (n t) -> p n t", t=4), gain_raw[:, :, 0].unsqueeze(1).to_broadcast([P, CHUNK, 4])
+        )
         y_planes = held([P, GROUPS, S], U8, "y_planes")
-        gain_bc = gain_sb[:]
         out_rows = out_0.rearrange("(g p t) j -> g p t j", g=GROUPS, t=4)
         out_words = out_1.rearrange("g p m i -> p g (m i)").bitcast(I32)
 
-        def first_stage(c, h_bf, v):
+        def first_stage(c, larger):
             h, u = divmod(c, HALF // CHUNK)
             cols = slice(u * CHUNK, (u + 1) * CHUNK)
-            all_cols = slice(c * CHUNK, (c + 1) * CHUNK)
             diff = psum.tile([P, 4, CHUNK], F32, name="diff", bufs=2)
             guess = psum.tile([P, 4, CHUNK], F32, name="guess", bufs=3)
-            for a in range(PASSES):
-                for t in range(4):
-                    m = slice(128 * t, 128 * (t + 1))
-                    nc.tensor.matmul_mx(
-                        guess[:, t, :], lhsT=wg_codes[:, a, m].bitcast(FP8X4), lhsT_scale=w_planes[4:, a, m],
-                        rhs=words[2, a, h][:, cols].bitcast(FP8X4), rhs_scale=planes[2][4 * a :, all_cols],
-                        start=(a == 0 and t == 0), stop=(a == PASSES - 1 and t == 3),
-                    )
+
+            def scale_of(l, a):
+                return planes[:, a, l * S + c * CHUNK : l * S + (c + 1) * CHUNK]
+
             for a in range(PASSES):
                 for t in range(4):
                     m = slice(128 * t, 128 * (t + 1))
                     nc.tensor.matmul_mx(
                         diff[:, t, :], lhsT=wa_codes[:, a, m].bitcast(FP8X4), lhsT_scale=wa_planes[:, a, m],
-                        rhs=words[0, a, h][:, cols].bitcast(FP8X4), rhs_scale=planes[0][4 * a :, all_cols],
+                        rhs=words[0, a, h][:, cols].bitcast(FP8X4), rhs_scale=scale_of(0, a),
                         start=(a == 0 and t == 0), stop=False,
                     )
+                for t in range(4):
+                    nc.tensor.matmul_mx(
+                        diff[:, t, :], lhsT=wq_codes[:, a, 256 * t : 256 * (t + 1)].bitcast(FP4X4),
+                        lhsT_scale=planes[:, a, 3 * S + 128 * t : 3 * S + 128 * (t + 1)],
+                        rhs=words[1, a, h][:, cols].bitcast(FP8X4), rhs_scale=scale_of(1, a),
+                        start=False, stop=(a == PASSES - 1 and t == 3),
+                    )
             for a in range(PASSES):
-                q_plane = planes[1] if a == 0 else q_planes_1
                 for t in range(4):
                     m = slice(128 * t, 128 * (t + 1))
                     nc.tensor.matmul_mx(
-                        diff[:, t, :], lhsT=wq_codes[:, a, 256 * t : 256 * (t + 1)].bitcast(FP4X4),
-                        lhsT_scale=w_planes[:, a, m],
-                        rhs=words[1, a, h][:, cols].bitcast(FP8X4), rhs_scale=q_plane[:, all_cols],
-                        start=False, stop=(a == PASSES - 1 and t == 3),
+                        guess[:, t, :], lhsT=wg_codes[:, a, m].bitcast(FP8X4),
+                        lhsT_scale=planes[:, a, 3 * S + H + 128 * t : 3 * S + H + 128 * (t + 1)],
+                        rhs=words[2, a, h][:, cols].bitcast(FP8X4), rhs_scale=scale_of(2, a),
+                        start=(a == 0 and t == 0), stop=(a == PASSES - 1 and t == 3),
                     )
-            success = ring.tile([P, CHUNK, 4], F32, name="success", bufs=3)
-            nc.scalar.activation(success[:], diff[:].rearrange("p t n -> p n t"), ACT.Sigmoid, scale=-1.0)
-            if c < 4:
-                larger = keep.tile([P, CHUNK, 4], F32, name="larger%d" % c, align_bytes=64)
+            if c < 3:
+                success = held([P, CHUNK, 4], F32, "success%d" % c)
             else:
-                larger = ring.tile([P, CHUNK, 4], F32, name="larger")
-            nc.vector.tensor_tensor(larger[:], guess[:].rearrange("p t n -> p n t"), success[:], ALU.max)
-            nc.vector.tensor_tensor(h_bf[:, v * CHUNK : (v + 1) * CHUNK, :], larger[:], gain_bc, ALU.mult)
+                success = ring.tile([P, CHUNK, 4], F32, name="success", bufs=3)
+            nc.scalar.activation(success[:], diff[:].rearrange("p t n -> p n t"), ACT.Sigmoid, scale=-1.0)
+            nc.vector.tensor_tensor(
+                larger.rearrange("p (n t) -> p n t", t=4), guess[:].rearrange("p t n -> p n t"), success[:], ALU.max
+            )
 
         h_mx, ys = {}, {}
 
@@ -214,7 +216,7 @@ def tile_list_guess_floor_mastery_kernel(
             width = STRIPS[w] * CHUNK
             h_codes = ring.tile([P, width], U32, name="h_codes", align_bytes=64, bufs=3)
             h_planes = ring.tile([P, width], U8, name="h_planes", align_bytes=64, bufs=3)
-            nc.vector.quantize_mx(h_codes[:].bitcast(FP8X4), h_planes[:], h_bf[:].rearrange("p n t -> p (n t)"))
+            nc.vector.quantize_mx(h_codes[:].bitcast(FP8X4), h_planes[:], h_bf[:].rearrange("p v e -> p (v e)"))
             h_mx[w] = (h_codes, h_planes)
 
         def second_stage(w):
@@ -222,7 +224,7 @@ def tile_list_guess_floor_mastery_kernel(
             cols = slice(FIRST[w] * CHUNK, FIRST[w] * CHUNK + width)
             h_codes, h_planes = h_mx[w]
             for g in range(GROUPS):
-                y = held([P, 4, width], F32, "y%d%d" % (w, g))
+                y = ring.tile([P, 4, width], F32, name="y", bufs=6)
                 ys[w, g] = y
                 per_bank = 512 // width
                 for pair in range(4 // per_bank):
@@ -241,6 +243,8 @@ def tile_list_guess_floor_mastery_kernel(
                         else:
                             nc.scalar.activation(y[:, t, :], logits[:, e, :], ACT.Identity, bias=bo_sb[:, g, t : t + 1])
                 nc.sync.dma_start(out_rows[g][:, :, cols], y[:])
+                if w == 0 and g == 0:
+                    quantize_wo(1)
 
         def result_planes(w):
             width = STRIPS[w] * CHUNK
@@ -262,16 +266,24 @@ def tile_list_guess_floor_mastery_kernel(
         wides = len(STRIPS)
         for w in range(wides + 2):
             if w < wides:
-                h_bf = held([P, STRIPS[w] * CHUNK, 4], BF16, "h_bf%d" % w)
+                h_bf = ring.tile([P, STRIPS[w], 4 * CHUNK], BF16, name="h_bf", align_bytes=64, bufs=2)
+                larger = ring.tile([P, STRIPS[w], 4 * CHUNK], F32, name="larger", bufs=2)
                 for v in range(STRIPS[w]):
-                    first_stage(FIRST[w] + v, h_bf, v)
+                    c = FIRST[w] + v
+                    first_stage(c, larger[:, v, :])
+                    if w not in WHOLE_GAIN:
+                        nc.gpsimd.tensor_tensor(h_bf[:, v, :], larger[:, v, :], gain_sb[:], ALU.mult)
+                if w in WHOLE_GAIN:
+                    nc.vector.tensor_tensor(
+                        h_bf[:], larger[:], gain_sb[:].unsqueeze(1).to_broadcast([P, STRIPS[w], 4 * CHUNK]), ALU.mult
+                    )
                 quantize_h(w, h_bf)
+                for v in range(STRIPS[w]):
+                    c = FIRST[w] + v
+                    if c < 3:
+                        gather(c, 1, 1, 1, "success%d" % c)
             if w == 0:
-                gather(1, [(0, 1)], "larger0")
-            if w == 0:
-                gather(1, [(1, 1)], "larger1")
-            if w == 0:
-                quantize_wo(1)
+                quantize_wo(0)
             if 0 <= w - 1 < wides:
                 second_stage(w - 1)
             if 0 <= w - 2 < wides:

@@ -26,6 +26,7 @@ STRIPS = (2, 2, 2, 2,)
 FIRST = [sum(STRIPS[:w]) for w in range(len(STRIPS))]
 OUT_ON_VECTOR = ()
 Y_ON_SCALAR = (0, 2, 4,)
+GAIN_ON_VECTOR = (7,)
 WHOLE_GAIN = ()
 
 
@@ -107,9 +108,9 @@ def tile_list_guess_floor_mastery_kernel(
             staged[ROW0:, : 3 * S].bitcast(I32), picked[ROW0:].rearrange("p l s -> p (l s)").bitcast(I32)
         )
         for a in range(PASSES):
-            for q in range(4):
-                row = ROW0 + 16 * a + 4 * q
-                nc.sync.dma_start(planes[32 * q : 32 * q + 4, a, :].bitcast(I32), staged[row : row + 4, :].bitcast(I32))
+            for r in range(4):
+                rows = slice(ROW0 + 16 * a + r, ROW0 + 16 * (a + 1), 4)
+                nc.sync.dma_start(planes[r:P:32, a, :].bitcast(I32), staged[rows, :].bitcast(I32))
         load_wo(0, "picked")
         words = {}
 
@@ -272,7 +273,8 @@ def tile_list_guess_floor_mastery_kernel(
                     c = FIRST[w] + v
                     first_stage(c, larger[:, v, :])
                     if w not in WHOLE_GAIN:
-                        nc.gpsimd.tensor_tensor(h_bf[:, v, :], larger[:, v, :], gain_sb[:], ALU.mult)
+                        engine = nc.vector if c in GAIN_ON_VECTOR else nc.gpsimd
+                        engine.tensor_tensor(h_bf[:, v, :], larger[:, v, :], gain_sb[:], ALU.mult)
                 if w in WHOLE_GAIN:
                     nc.vector.tensor_tensor(
                         h_bf[:], larger[:], gain_sb[:].unsqueeze(1).to_broadcast([P, STRIPS[w], 4 * CHUNK]), ALU.mult
@@ -289,8 +291,7 @@ def tile_list_guess_floor_mastery_kernel(
             if 0 <= w - 2 < wides:
                 result_planes(w - 2)
 
-        for q in range(4):
+        for r in range(4):
             nc.sync.dma_start(
-                out_2[:, 4 * q : 4 * q + 4, :].rearrange("g r m -> r g m").bitcast(I32),
-                y_planes[32 * q : 32 * q + 4].bitcast(I32),
+                out_2[:, r:16:4, :].rearrange("g q m -> q g m").bitcast(I32), y_planes[r:P:32].bitcast(I32)
             )

@@ -154,8 +154,8 @@ def tile_list_guess_floor_mastery_kernel(
 
         def quantize_wo(g):
             wo_bf = held([P, 4, 128, 4], BF16, "wo_bf%d" % g, "wa_bf%d" % g)
-            dst = wo_bf[:].rearrange("p t m j -> p m t j")
-            src = wo_raw[g][:].rearrange("p j (m t) -> p m t j", t=4)
+            dst = wo_bf[:].rearrange("p t m j -> p m j t")
+            src = wo_raw[g][:].rearrange("p j (m t) -> p m j t", t=4)
             for m in range(0, 128, 32):
                 nc.scalar.copy(dst[:, m : m + 32], src[:, m : m + 32])
             nc.vector.quantize_mx(

@@ -253,8 +253,8 @@ def tile_list_guess_floor_mastery_kernel(
             y_codes = held([P, GROUPS, width], I32, "y_codes%d" % w)
             for g in range(GROUPS):
                 y_bf = ring.tile([P, width, 4], BF16, name="y_bf", align_bytes=64, bufs=3)
-                dst = y_bf[:]
-                src = ys[w, g][:].rearrange("p t n -> p n t")
+                dst = y_bf[:].rearrange("p (c i) t -> p c t i", i=2)
+                src = ys[w, g][:].rearrange("p t (c i) -> p c t i", i=2)
                 if GROUPS * w + g in Y_ON_SCALAR:
                     nc.scalar.copy(dst, src)
                 else:

@@ -142,7 +142,7 @@ def tile_list_guess_floor_mastery_kernel(
             (wq_codes[:].bitcast(I32), wq_raw[:], 4),
             (wg_codes[:], wg_raw[:], 8),
         ):
-            nc.vector.tensor_copy(
+            nc.gpsimd.tensor_copy(
                 dst.rearrange("p a (t b w) -> p a t b w", t=4, w=run),
                 src.rearrange("p a (b t w) -> p a t b w", t=4, w=run),
             )
@@ -262,7 +262,10 @@ def tile_list_guess_floor_mastery_kernel(
                 nc.vector.quantize_mx(
                     y_codes[:, g, :].bitcast(FP8X4), y_planes[:, g, cols], y_bf[:].rearrange("p n t -> p (n t)")
                 )
-            nc.sync.dma_start(out_words[:, :, cols], y_codes[:])
+                if w == len(STRIPS) - 1:
+                    nc.sync.dma_start(out_words[:, g, cols], y_codes[:, g, :])
+            if w < len(STRIPS) - 1:
+                nc.sync.dma_start(out_words[:, :, cols], y_codes[:])
 
         wides = len(STRIPS)
         for w in range(wides + 2):
@@ -292,6 +295,6 @@ def tile_list_guess_floor_mastery_kernel(
                 result_planes(w - 2)
 
         for r in range(4):
-            nc.sync.dma_start(
+            (nc.sync, nc.scalar)[r % 2].dma_start(
                 out_2[:, r:16:4, :].rearrange("g q m -> q g m").bitcast(I32), y_planes[r:P:32].bitcast(I32)
             )

@@ -100,7 +100,7 @@ def tile_list_guess_floor_mastery_kernel(
 
         for l in range(3):
             nc.vector.tensor_copy(picked[:, l, :], tab_rows[:].indirect(lists[l][:]))
-        nc.vector.tensor_copy(
+        nc.gpsimd.tensor_copy(
             staged[ROW0:, 3 * S :].bitcast(I32).rearrange("p (i t b w) -> p i t b w", i=2, t=4, w=2),
             w_rows[ROW0:].bitcast(I32).rearrange("p i (b t w) -> p i t b w", t=4, w=2),
         )
@@ -154,15 +154,16 @@ def tile_list_guess_floor_mastery_kernel(
 
         def quantize_wo(g):
             wo_bf = held([P, 4, 128, 4], BF16, "wo_bf%d" % g, "wa_bf%d" % g)
-            dst = wo_bf[:].rearrange("p t m j -> p m j t")
-            src = wo_raw[g][:].rearrange("p j (m t) -> p m j t", t=4)
-            for m in range(0, 128, 32):
-                nc.scalar.copy(dst[:, m : m + 32], src[:, m : m + 32])
+            dst = wo_bf[:].rearrange("p (u i) m j -> p u m j i", i=2)
+            src = wo_raw[g][:].rearrange("p j (m u i) -> p u m j i", u=2, i=2)
+            for m in range(0, 128, 64):
+                for u in range(2):
+                    nc.scalar.copy(dst[:, u, m : m + 64], src[:, u, m : m + 64])
             nc.vector.quantize_mx(
                 wo_codes[:, g, :].bitcast(FP8X4), wo_planes[:, g, :], wo_bf[:].rearrange("p t m j -> p (t m j)")
             )
 
-        nc.scalar.copy(
+        nc.gpsimd.tensor_copy(
             gain_sb[:].rearrange("p (n t) -> p n t", t=4), gain_raw[:, :, 0].unsqueeze(1).to_broadcast([P, CHUNK, 4])
         )
         y_planes = held([P, GROUPS, S], U8, "y_planes")

@@ -56,12 +56,9 @@ def tile_list_guess_floor_mastery_kernel(
         gain_sb = held([P, CHUNK * 4], F32, "gain_sb")
         gain_raw = held([P, 4, 8], F32, "gain_raw")
         bo_sb = held([P, GROUPS, 4], F32, "bo_sb")
-        warm = held([P, 2], F32, "warm")
 
         nc.vector.memset(tab_rows[0:ROW0, :].bitcast(I32), 0)
-        nc.vector.memset(warm[:, 0:1], 0.0)
         nc.vector.memset(planes[:].rearrange("p a e -> p (a e)").bitcast(I32), 0)
-        nc.scalar.activation(warm[:, 1:2], warm[:, 0:1], ACT.Sigmoid)
 
         def load_tab(a):
             nc.sync.dma_start(tab[a][:], tab_words[a].rearrange("p t i -> p (t i)").bitcast(I32))

@@ -46,9 +46,9 @@ def tile_list_guess_floor_mastery_kernel(
         lists = [held([P, S // 16], U16, "list%d" % l) for l in range(3)]
         tab = [held([P, T], I32, "tab%d" % a) for a in range(PASSES)]
         tab_rows = held([P, T], U8, "tab_rows")
-        w_rows = held([P, 2, H], U8, "w_rows")
-        staged = held([P, 3 * S + 2 * H], U8, "staged")
-        planes = held([P, PASSES, 3 * S + 2 * H], U8, "planes")
+        w_rows = held([P, 2, PASSES, H], U8, "w_rows")
+        w_planes = held([P, 2, PASSES, H], U8, "w_planes")
+        planes = held([P, PASSES, 3 * S], U8, "planes")
         wa_raw = [held([P, 4, H], F32, "wa_raw%d" % a) for a in range(PASSES)]
         picked = held([P, 3, S], U8, "picked")
         wq_raw = held([P, PASSES, H // 2], I32, "wq_raw")
@@ -57,6 +57,7 @@ def tile_list_guess_floor_mastery_kernel(
         gain_raw = held([P, 4, 8], F32, "gain_raw")
         bo_sb = held([P, GROUPS, 4], F32, "bo_sb")
 
+        nc.gpsimd.memset(w_rows[:].rearrange("p i a e -> p (i a e)").bitcast(I32), 0)
         nc.vector.memset(tab_rows[0:ROW0, :].bitcast(I32), 0)
         nc.vector.memset(planes[:].rearrange("p a e -> p (a e)").bitcast(I32), 0)
 
@@ -81,34 +82,40 @@ def tile_list_guess_floor_mastery_kernel(
         nc.sync.dma_start(tab_rows[ROW0:, :].bitcast(I32), tab_scales.rearrange("a q t -> (a q) t").bitcast(I32))
         for l, src in enumerate((offs, offs2, offs3)):
             nc.sync.dma_start(lists[l][:], src)
-        for i, src in enumerate((wq_scales, wg_scales)):
-            nc.sync.dma_start(w_rows[ROW0:, i, :].bitcast(I32), src.rearrange("a q e -> (a q) e").bitcast(I32))
+
+        def load_w_rows(i, r):
+            src = (wq_scales, wg_scales)[i]
+            nc.sync.dma_start(
+                w_rows[r:P:32, i].bitcast(I32), src[:, r:16:4, :].rearrange("a q e -> q a e").bitcast(I32)
+            )
+
         load_wa(0)
         load_tab(0)
-        load_gain(0)
-        load_gain(1)
+        for r in range(4):
+            load_w_rows(0, r)
+        load_w_rows(1, 0)
+        load_w_rows(1, 1)
         load_wa(1)
-        load_gain(2)
-        load_gain(3)
+        load_w_rows(1, 2)
         nc.sync.dma_start(wq_raw[:], wq_words.rearrange("a p e -> p a e").bitcast(I32))
         nc.sync.dma_start(wg_raw[:], wg_words.rearrange("a p e i -> p a (e i)").bitcast(I32))
+        load_w_rows(1, 3)
+        for t in range(4):
+            load_gain(t)
         load_tab(1)
         nc.sync.dma_start(bo_sb[:], bo.rearrange("(g p t) -> p g t", g=GROUPS, t=4))
 
         for l in range(3):
             nc.vector.tensor_copy(picked[:, l, :], tab_rows[:].indirect(lists[l][:]))
         nc.gpsimd.tensor_copy(
-            staged[ROW0:, 3 * S :].bitcast(I32).rearrange("p (i t b w) -> p i t b w", i=2, t=4, w=2),
-            w_rows[ROW0:].bitcast(I32).rearrange("p i (b t w) -> p i t b w", t=4, w=2),
-        )
-        nc.vector.tensor_copy(
-            staged[ROW0:, : 3 * S].bitcast(I32), picked[ROW0:].rearrange("p l s -> p (l s)").bitcast(I32)
+            w_planes[:].bitcast(I32).rearrange("p i a (t b w) -> p (i a) t b w", t=4, w=2),
+            w_rows[:].bitcast(I32).rearrange("p i a (b t w) -> p (i a) t b w", t=4, w=2),
         )
         for a in range(PASSES):
             for r in range(4):
                 rows = slice(ROW0 + 16 * a + r, ROW0 + 16 * (a + 1), 4)
-                nc.sync.dma_start(planes[r:P:32, a, :].bitcast(I32), staged[rows, :].bitcast(I32))
-        load_wo(0, "picked")
+                nc.sync.dma_start(planes[r:P:32, a, :].bitcast(I32), picked[rows].rearrange("p l s -> p (l s)").bitcast(I32))
+        load_wo(0, "tab_rows")
         words = {}
 
         def gather(l, a, first, count, tag):
@@ -187,7 +194,7 @@ def tile_list_guess_floor_mastery_kernel(
                 for t in range(4):
                     nc.tensor.matmul_mx(
                         diff[:, t, :], lhsT=wq_codes[:, a, 256 * t : 256 * (t + 1)].bitcast(FP4X4),
-                        lhsT_scale=planes[:, a, 3 * S + 128 * t : 3 * S + 128 * (t + 1)],
+                        lhsT_scale=w_planes[:, 0, a, 128 * t : 128 * (t + 1)],
                         rhs=words[1, a, h][:, cols].bitcast(FP8X4), rhs_scale=scale_of(1, a),
                         start=False, stop=(a == PASSES - 1 and t == 3),
                     )
@@ -196,7 +203,7 @@ def tile_list_guess_floor_mastery_kernel(
                     m = slice(128 * t, 128 * (t + 1))
                     nc.tensor.matmul_mx(
                         guess[:, t, :], lhsT=wg_codes[:, a, m].bitcast(FP8X4),
-                        lhsT_scale=planes[:, a, 3 * S + H + 128 * t : 3 * S + H + 128 * (t + 1)],
+                        lhsT_scale=w_planes[:, 1, a, m],
                         rhs=words[2, a, h][:, cols].bitcast(FP8X4), rhs_scale=scale_of(2, a),
                         start=(a == 0 and t == 0), stop=(a == PASSES - 1 and t == 3),
                     )

@@ -97,13 +97,12 @@ def tile_list_guess_floor_mastery_kernel(
         load_w_rows(1, 1)
         load_wa(1)
         load_w_rows(1, 2)
-        nc.sync.dma_start(wq_raw[:], wq_words.rearrange("a p e -> p a e").bitcast(I32))
-        nc.sync.dma_start(wg_raw[:], wg_words.rearrange("a p e i -> p a (e i)").bitcast(I32))
         load_w_rows(1, 3)
+        load_tab(1)
         for t in range(4):
             load_gain(t)
-        load_tab(1)
-        nc.sync.dma_start(bo_sb[:], bo.rearrange("(g p t) -> p g t", g=GROUPS, t=4))
+        nc.sync.dma_start(wq_raw[:], wq_words.rearrange("a p e -> p a e").bitcast(I32))
+        nc.sync.dma_start(wg_raw[:], wg_words.rearrange("a p e i -> p a (e i)").bitcast(I32))
 
         for l in range(3):
             nc.vector.tensor_copy(picked[:, l, :], tab_rows[:].indirect(lists[l][:]))
@@ -116,6 +115,7 @@ def tile_list_guess_floor_mastery_kernel(
                 rows = slice(ROW0 + 16 * a + r, ROW0 + 16 * (a + 1), 4)
                 nc.sync.dma_start(planes[r:P:32, a, :].bitcast(I32), picked[rows].rearrange("p l s -> p (l s)").bitcast(I32))
         load_wo(0, "tab_rows")
+        nc.sync.dma_start(bo_sb[:], bo.rearrange("(g p t) -> p g t", g=GROUPS, t=4))
         words = {}
 
         def gather(l, a, first, count, tag):
@@ -152,6 +152,8 @@ def tile_list_guess_floor_mastery_kernel(
             )
         for l in range(3):
             gather(l, 1, 0, 1, None)
+        for l in range(2):
+            gather(l, 1, 1, 1, None)
 
         wo_codes = held([P, GROUPS, 512], U32, "wo_codes")
         wo_planes = held([P, GROUPS, 512], U8, "wo_planes")
@@ -207,7 +209,7 @@ def tile_list_guess_floor_mastery_kernel(
                         rhs=words[2, a, h][:, cols].bitcast(FP8X4), rhs_scale=scale_of(2, a),
                         start=(a == 0 and t == 0), stop=(a == PASSES - 1 and t == 3),
                     )
-            if c < 3:
+            if c == 1:
                 success = held([P, CHUNK, 4], F32, "success%d" % c)
             else:
                 success = ring.tile([P, CHUNK, 4], F32, name="success", bufs=3)
@@ -290,8 +292,8 @@ def tile_list_guess_floor_mastery_kernel(
                 quantize_h(w, h_bf)
                 for v in range(STRIPS[w]):
                     c = FIRST[w] + v
-                    if c < 3:
-                        gather(c, 1, 1, 1, "success%d" % c)
+                    if c == 1:
+                        gather(2, 1, 1, 1, "success%d" % c)
             if w == 0:
                 quantize_wo(0)
             if 0 <= w - 1 < wides:

@@ -89,8 +89,8 @@ def tile_list_guess_floor_mastery_kernel(
                 w_rows[r:P:32, i].bitcast(I32), src[:, r:16:4, :].rearrange("a q e -> q a e").bitcast(I32)
             )
 
-        load_wa(0)
         load_tab(0)
+        load_wa(0)
         for r in range(4):
             load_w_rows(0, r)
         load_w_rows(1, 0)
@@ -102,7 +102,6 @@ def tile_list_guess_floor_mastery_kernel(
         for t in range(4):
             load_gain(t)
         nc.sync.dma_start(wq_raw[:], wq_words.rearrange("a p e -> p a e").bitcast(I32))
-        nc.sync.dma_start(wg_raw[:], wg_words.rearrange("a p e i -> p a (e i)").bitcast(I32))
 
         for l in range(3):
             nc.vector.tensor_copy(picked[:, l, :], tab_rows[:].indirect(lists[l][:]))
@@ -114,6 +113,8 @@ def tile_list_guess_floor_mastery_kernel(
             for r in range(4):
                 rows = slice(ROW0 + 16 * a + r, ROW0 + 16 * (a + 1), 4)
                 nc.sync.dma_start(planes[r:P:32, a, :].bitcast(I32), picked[rows].rearrange("p l s -> p (l s)").bitcast(I32))
+                if a == 0 and r == 0:
+                    nc.sync.dma_start(wg_raw[:], wg_words.rearrange("a p e i -> p a (e i)").bitcast(I32))
         load_wo(0, "tab_rows")
         nc.sync.dma_start(bo_sb[:], bo.rearrange("(g p t) -> p g t", g=GROUPS, t=4))
         words = {}

@@ -21,13 +21,13 @@ PASSES = K // 512
 GROUPS = N // 512
 HALF = 512
 ROW0 = 96
+STRIP = 256
+STRIPS = S // STRIP
 CHUNK = 128
-STRIPS = (2, 2, 2, 2,)
-FIRST = [sum(STRIPS[:w]) for w in range(len(STRIPS))]
-OUT_ON_VECTOR = ()
-Y_ON_SCALAR = (0, 2, 4,)
-GAIN_ON_VECTOR = (7,)
-WHOLE_GAIN = ()
+ROUND_ON_SCALAR = (6,)
+ROUND_BEHIND = {0: "success31", 1: "h_bf2", 2: "success30", 3: "h_bf3"}
+GAIN_ON_VECTOR = ()
+LOGIT_BANKS = (0, 1, 0, 1, 2, 3, 4, 5, 0, 1, 6, 7, 2, 3, 4, 5)
 
 
 def tile_list_guess_floor_mastery_kernel(
@@ -37,7 +37,6 @@ def tile_list_guess_floor_mastery_kernel(
     nc = tc.nc
     with ExitStack() as ctx:
         keep = ctx.enter_context(tc.tile_pool(name="keep", bufs=1))
-        ring = ctx.enter_context(tc.tile_pool(name="ring", bufs=2))
         psum = ctx.enter_context(tc.psum_pool(name="psum", bufs=1))
 
         def held(shape, dtype, name, tag=None):
@@ -48,8 +47,9 @@ def tile_list_guess_floor_mastery_kernel(
         tab_rows = held([P, T], U8, "tab_rows")
         w_rows = held([P, 2, PASSES, H], U8, "w_rows")
         w_planes = held([P, 2, PASSES, H], U8, "w_planes")
-        planes = held([P, PASSES, 3 * S], U8, "planes")
+        planes = [[held([P, 3 * HALF], U8, "planes%d%d" % (h, a)) for a in range(PASSES)] for h in range(2)]
         wa_raw = [held([P, 4, H], F32, "wa_raw%d" % a) for a in range(PASSES)]
+        wo_raw = [held([P, 4, 512], F32, "wo_raw%d" % g) for g in range(GROUPS)]
         picked = held([P, 3, S], U8, "picked")
         wq_raw = held([P, PASSES, H // 2], I32, "wq_raw")
         wg_raw = held([P, PASSES, H], I32, "wg_raw")
@@ -59,7 +59,9 @@ def tile_list_guess_floor_mastery_kernel(
 
         nc.gpsimd.memset(w_rows[:].rearrange("p i a e -> p (i a e)").bitcast(I32), 0)
         nc.vector.memset(tab_rows[0:ROW0, :].bitcast(I32), 0)
-        nc.vector.memset(planes[:].rearrange("p a e -> p (a e)").bitcast(I32), 0)
+        for h, engine in enumerate((nc.vector, nc.gpsimd)):
+            for a in range(PASSES):
+                engine.memset(planes[h][a][:].bitcast(I32), 0)
 
         def load_tab(a):
             nc.sync.dma_start(tab[a][:], tab_words[a].rearrange("p t i -> p (t i)").bitcast(I32))
@@ -72,16 +74,9 @@ def tile_list_guess_floor_mastery_kernel(
                 nc.sync.dma_start(gain_raw[:, t, 0:1], gain.rearrange("(b t q) -> t b q", t=4, q=8)[t].unsqueeze(2))
 
         wo_rows = wo.rearrange("(b t q) n -> t b q n", t=4, q=8)
-        wo_raw = {}
 
-        def load_wo(g, tag):
-            wo_raw[g] = held([P, 4, 512], F32, "wo_raw%d" % g, tag)
-            for t in range(4):
-                nc.sync.dma_start(wo_raw[g][:, t, :], wo_rows[t][:, :, 512 * g : 512 * (g + 1)])
-
-        nc.sync.dma_start(tab_rows[ROW0:, :].bitcast(I32), tab_scales.rearrange("a q t -> (a q) t").bitcast(I32))
-        for l, src in enumerate((offs, offs2, offs3)):
-            nc.sync.dma_start(lists[l][:], src)
+        def load_wo(g, t):
+            nc.sync.dma_start(wo_raw[g][:, t, :], wo_rows[t][:, :, 512 * g : 512 * (g + 1)])
 
         def load_w_rows(i, r):
             src = (wq_scales, wg_scales)[i]
@@ -89,6 +84,16 @@ def tile_list_guess_floor_mastery_kernel(
                 w_rows[r:P:32, i].bitcast(I32), src[:, r:16:4, :].rearrange("a q e -> q a e").bitcast(I32)
             )
 
+        def move_plane(h, a, r):
+            rows = slice(ROW0 + 16 * a + r, ROW0 + 16 * (a + 1), 4)
+            nc.sync.dma_start(
+                planes[h][a][r:P:32, :].bitcast(I32).rearrange("p (l e) -> p l e", l=3),
+                picked[rows, :, HALF * h : HALF * (h + 1)].bitcast(I32),
+            )
+
+        nc.sync.dma_start(tab_rows[ROW0:, :].bitcast(I32), tab_scales.rearrange("a q t -> (a q) t").bitcast(I32))
+        for l, src in enumerate((offs, offs2, offs3)):
+            nc.sync.dma_start(lists[l][:], src)
         load_tab(0)
         load_wa(0)
         for r in range(4):
@@ -99,8 +104,6 @@ def tile_list_guess_floor_mastery_kernel(
         load_w_rows(1, 2)
         load_w_rows(1, 3)
         load_tab(1)
-        for t in range(4):
-            load_gain(t)
         nc.sync.dma_start(wq_raw[:], wq_words.rearrange("a p e -> p a e").bitcast(I32))
 
         for l in range(3):
@@ -109,17 +112,27 @@ def tile_list_guess_floor_mastery_kernel(
             w_planes[:].bitcast(I32).rearrange("p i a (t b w) -> p (i a) t b w", t=4, w=2),
             w_rows[:].bitcast(I32).rearrange("p i a (b t w) -> p (i a) t b w", t=4, w=2),
         )
+        nc.sync.dma_start(bo_sb[:], bo.rearrange("(g p t) -> p g t", g=GROUPS, t=4))
+        for r in range(4):
+            move_plane(0, 0, r)
+        load_wo(0, 0)
+        load_wo(0, 1)
+        for r in range(4):
+            move_plane(0, 1, r)
+        load_wo(0, 2)
+        load_wo(0, 3)
+        nc.sync.dma_start(wg_raw[:], wg_words.rearrange("a p e i -> p a (e i)").bitcast(I32))
+        for t in range(4):
+            load_gain(t)
+        for t in range(4):
+            load_wo(1, t)
         for a in range(PASSES):
             for r in range(4):
-                rows = slice(ROW0 + 16 * a + r, ROW0 + 16 * (a + 1), 4)
-                nc.sync.dma_start(planes[r:P:32, a, :].bitcast(I32), picked[rows].rearrange("p l s -> p (l s)").bitcast(I32))
-                if a == 0 and r == 0:
-                    nc.sync.dma_start(wg_raw[:], wg_words.rearrange("a p e i -> p a (e i)").bitcast(I32))
-        load_wo(0, "tab_rows")
-        nc.sync.dma_start(bo_sb[:], bo.rearrange("(g p t) -> p g t", g=GROUPS, t=4))
+                move_plane(1, a, r)
+
         words = {}
 
-        def gather(l, a, first, count, tag):
+        def gather(l, a, first, count, tag=None):
             room = held([P, count * HALF], U32, "room%d%d%d" % (l, a, first), tag)
             cols = slice(first * HALF // 16, (first + count) * HALF // 16)
             nc.vector.tensor_copy(room[:], tab[a][:].bitcast(U32).indirect(lists[l][:, cols]))
@@ -127,7 +140,7 @@ def tile_list_guess_floor_mastery_kernel(
                 words[l, a, first + i] = room[:, i * HALF : (i + 1) * HALF]
 
         for l in range(3):
-            gather(l, 0, 0, 2, None)
+            gather(l, 0, 0, 2)
 
         wa_codes = held([P, PASSES, H], U32, "wa_codes")
         wa_planes = held([P, PASSES, H], U8, "wa_planes")
@@ -141,26 +154,28 @@ def tile_list_guess_floor_mastery_kernel(
             )
 
         wq_codes = held([P, PASSES, 2 * H], U8, "wq_codes")
-        wg_codes = held([P, PASSES, H], I32, "wg_codes")
-        load_wo(1, "wa_raw1")
-        for dst, src, run in (
-            (wq_codes[:].bitcast(I32), wq_raw[:], 4),
-            (wg_codes[:], wg_raw[:], 8),
-        ):
+        wg_codes = [held([P, PASSES, H // 2], I32, "wg_codes%d" % u) for u in range(2)]
+        nc.gpsimd.tensor_copy(
+            wq_codes[:].bitcast(I32).rearrange("p a (t b w) -> p a t b w", t=4, w=4),
+            wq_raw[:].rearrange("p a (b t w) -> p a t b w", t=4, w=4),
+        )
+        for u in range(2):
             nc.gpsimd.tensor_copy(
-                dst.rearrange("p a (t b w) -> p a t b w", t=4, w=run),
-                src.rearrange("p a (b t w) -> p a t b w", t=4, w=run),
+                wg_codes[u][:].rearrange("p a (i b w) -> p a i b w", i=2, w=8),
+                wg_raw[:].rearrange("p a (b t w) -> p a t b w", t=4, w=8)[:, :, 2 * u : 2 * u + 2],
             )
-        for l in range(3):
-            gather(l, 1, 0, 1, None)
-        for l in range(2):
-            gather(l, 1, 1, 1, None)
+        for h in range(2):
+            for l in range(3 - h):
+                gather(l, 1, h, 1)
+        nc.gpsimd.tensor_copy(
+            gain_sb[:].rearrange("p (n t) -> p n t", t=4), gain_raw[:, :, 0].unsqueeze(1).to_broadcast([P, CHUNK, 4])
+        )
 
         wo_codes = held([P, GROUPS, 512], U32, "wo_codes")
         wo_planes = held([P, GROUPS, 512], U8, "wo_planes")
 
         def quantize_wo(g):
-            wo_bf = held([P, 4, 128, 4], BF16, "wo_bf%d" % g, "wa_bf%d" % g)
+            wo_bf = held([P, 4, 128, 4], BF16, "wo_bf%d" % g)
             dst = wo_bf[:].rearrange("p (u i) m j -> p u m j i", i=2)
             src = wo_raw[g][:].rearrange("p j (m u i) -> p u m j i", u=2, i=2)
             for m in range(0, 128, 64):
@@ -170,137 +185,128 @@ def tile_list_guess_floor_mastery_kernel(
                 wo_codes[:, g, :].bitcast(FP8X4), wo_planes[:, g, :], wo_bf[:].rearrange("p t m j -> p (t m j)")
             )
 
-        nc.gpsimd.tensor_copy(
-            gain_sb[:].rearrange("p (n t) -> p n t", t=4), gain_raw[:, :, 0].unsqueeze(1).to_broadcast([P, CHUNK, 4])
-        )
         y_planes = held([P, GROUPS, S], U8, "y_planes")
         out_rows = out_0.rearrange("(g p t) j -> g p t j", g=GROUPS, t=4)
         out_words = out_1.rearrange("g p m i -> p g (m i)").bitcast(I32)
 
-        def first_stage(c, larger):
-            h, u = divmod(c, HALF // CHUNK)
-            cols = slice(u * CHUNK, (u + 1) * CHUNK)
-            diff = psum.tile([P, 4, CHUNK], F32, name="diff", bufs=2)
-            guess = psum.tile([P, 4, CHUNK], F32, name="guess", bufs=3)
+        def moving(l, a, w):
+            h, v = divmod(w, HALF // STRIP)
+            first = l * HALF + v * STRIP
+            return words[l, a, h][:, v * STRIP : (v + 1) * STRIP].bitcast(FP8X4), planes[h][a][:, first : first + STRIP]
 
-            def scale_of(l, a):
-                return planes[:, a, l * S + c * CHUNK : l * S + (c + 1) * CHUNK]
+        success = {}
 
+        def difference(w, u):
+            diff = psum.tile([P, 2, STRIP], F32, name="diff", tag="bank%d" % ((2 * w + u) % 4))
             for a in range(PASSES):
-                for t in range(4):
-                    m = slice(128 * t, 128 * (t + 1))
+                for i in range(2):
+                    m = slice(128 * (2 * u + i), 128 * (2 * u + i + 1))
                     nc.tensor.matmul_mx(
-                        diff[:, t, :], lhsT=wa_codes[:, a, m].bitcast(FP8X4), lhsT_scale=wa_planes[:, a, m],
-                        rhs=words[0, a, h][:, cols].bitcast(FP8X4), rhs_scale=scale_of(0, a),
-                        start=(a == 0 and t == 0), stop=False,
+                        diff[:, i, :], lhsT=wa_codes[:, a, m].bitcast(FP8X4), lhsT_scale=wa_planes[:, a, m],
+                        rhs=moving(0, a, w)[0], rhs_scale=moving(0, a, w)[1],
+                        start=(a == 0 and i == 0), stop=False,
                     )
-                for t in range(4):
+                for i in range(2):
+                    t = 2 * u + i
                     nc.tensor.matmul_mx(
-                        diff[:, t, :], lhsT=wq_codes[:, a, 256 * t : 256 * (t + 1)].bitcast(FP4X4),
+                        diff[:, i, :], lhsT=wq_codes[:, a, 256 * t : 256 * (t + 1)].bitcast(FP4X4),
                         lhsT_scale=w_planes[:, 0, a, 128 * t : 128 * (t + 1)],
-                        rhs=words[1, a, h][:, cols].bitcast(FP8X4), rhs_scale=scale_of(1, a),
-                        start=False, stop=(a == PASSES - 1 and t == 3),
+                        rhs=moving(1, a, w)[0], rhs_scale=moving(1, a, w)[1],
+                        start=False, stop=(a == PASSES - 1 and i == 1),
                     )
+            success[w, u] = held([P, STRIP, 2], F32, "success%d%d" % (w, u))
+            nc.scalar.activation(success[w, u][:], diff[:].rearrange("p i n -> p n i"), ACT.Sigmoid, scale=-1.0)
+
+        def guess_floor(w, u, larger):
+            guess = psum.tile([P, 2, STRIP], F32, name="guess", tag="bank%d" % (4 + (2 * w + u) % 4))
             for a in range(PASSES):
-                for t in range(4):
-                    m = slice(128 * t, 128 * (t + 1))
+                for i in range(2):
+                    m = slice(128 * (2 * u + i), 128 * (2 * u + i + 1))
                     nc.tensor.matmul_mx(
-                        guess[:, t, :], lhsT=wg_codes[:, a, m].bitcast(FP8X4),
-                        lhsT_scale=w_planes[:, 1, a, m],
-                        rhs=words[2, a, h][:, cols].bitcast(FP8X4), rhs_scale=scale_of(2, a),
-                        start=(a == 0 and t == 0), stop=(a == PASSES - 1 and t == 3),
+                        guess[:, i, :], lhsT=wg_codes[u][:, a, 128 * i : 128 * (i + 1)].bitcast(FP8X4), lhsT_scale=w_planes[:, 1, a, m],
+                        rhs=moving(2, a, w)[0], rhs_scale=moving(2, a, w)[1],
+                        start=(a == 0 and i == 0), stop=(a == PASSES - 1 and i == 1),
                     )
-            if c == 1:
-                success = held([P, CHUNK, 4], F32, "success%d" % c)
-            else:
-                success = ring.tile([P, CHUNK, 4], F32, name="success", bufs=3)
-            nc.scalar.activation(success[:], diff[:].rearrange("p t n -> p n t"), ACT.Sigmoid, scale=-1.0)
-            nc.vector.tensor_tensor(
-                larger.rearrange("p (n t) -> p n t", t=4), guess[:].rearrange("p t n -> p n t"), success[:], ALU.max
-            )
+            nc.vector.tensor_tensor(larger[:, u], guess[:].rearrange("p i n -> p n i"), success[w, u][:], ALU.max)
 
-        h_mx, ys = {}, {}
+        h_mx = {}
 
-        def quantize_h(w, h_bf):
-            width = STRIPS[w] * CHUNK
-            h_codes = ring.tile([P, width], U32, name="h_codes", align_bytes=64, bufs=3)
-            h_planes = ring.tile([P, width], U8, name="h_planes", align_bytes=64, bufs=3)
-            nc.vector.quantize_mx(h_codes[:].bitcast(FP8X4), h_planes[:], h_bf[:].rearrange("p v e -> p (v e)"))
+        def make_h(w):
+            larger = held([P, 2, STRIP, 2], F32, "larger%d" % w, "h_bf%d" % (w - 2) if w >= 2 else None)
+            for u in range(2):
+                guess_floor(w, u, larger)
+            h_bf = held([P, STRIP // CHUNK, CHUNK, 2, 2], BF16, "h_bf%d" % w)
+            for c in range(STRIP // CHUNK):
+                (nc.vector if (w, c) in GAIN_ON_VECTOR else nc.gpsimd).tensor_tensor(
+                    h_bf[:, c],
+                    larger[:, :, CHUNK * c : CHUNK * (c + 1), :].rearrange("p u n i -> p n u i"),
+                    gain_sb[:].rearrange("p (n u i) -> p n u i", u=2, i=2),
+                    ALU.mult,
+                )
+            h_codes = held([P, STRIP], U32, "h_codes%d" % w)
+            h_planes = held([P, STRIP], U8, "h_planes%d" % w)
+            nc.vector.quantize_mx(h_codes[:].bitcast(FP8X4), h_planes[:], h_bf[:].rearrange("p c n u i -> p (c n u i)"))
             h_mx[w] = (h_codes, h_planes)
 
-        def second_stage(w):
-            width = STRIPS[w] * CHUNK
-            cols = slice(FIRST[w] * CHUNK, FIRST[w] * CHUNK + width)
+        ys = {}
+
+        def second_stage(w, g):
+            cols = slice(w * STRIP, (w + 1) * STRIP)
             h_codes, h_planes = h_mx[w]
-            for g in range(GROUPS):
-                y = ring.tile([P, 4, width], F32, name="y", bufs=6)
-                ys[w, g] = y
-                per_bank = 512 // width
-                for pair in range(4 // per_bank):
-                    logits = psum.tile([P, per_bank, width], F32, name="logits", bufs=3)
-                    for e in range(per_bank):
-                        t = per_bank * pair + e
-                        m = slice(128 * t, 128 * (t + 1))
-                        nc.tensor.matmul_mx(
-                            logits[:, e, :], lhsT=wo_codes[:, g, m].bitcast(FP8X4), lhsT_scale=wo_planes[:, g, m],
-                            rhs=h_codes[:].bitcast(FP8X4), rhs_scale=h_planes[:], start=True, stop=True,
-                        )
-                    for e in range(per_bank):
-                        t = per_bank * pair + e
-                        if (w, g, pair) in OUT_ON_VECTOR:
-                            nc.vector.tensor_scalar(y[:, t, :], logits[:, e, :], bo_sb[:, g, t : t + 1], None, ALU.add)
-                        else:
-                            nc.scalar.activation(y[:, t, :], logits[:, e, :], ACT.Identity, bias=bo_sb[:, g, t : t + 1])
-                nc.sync.dma_start(out_rows[g][:, :, cols], y[:])
-                if w == 0 and g == 0:
-                    quantize_wo(1)
+            y = held([P, 4, STRIP], F32, "y%d%d" % (w, g))
+            ys[w, g] = y
+            for pair in range(2):
+                j = 2 * (GROUPS * w + g) + pair
+                logits = psum.tile([P, 2, STRIP], F32, name="logits", tag="bank%d" % LOGIT_BANKS[j])
+                for e in range(2):
+                    m = slice(128 * (2 * pair + e), 128 * (2 * pair + e + 1))
+                    nc.tensor.matmul_mx(
+                        logits[:, e, :], lhsT=wo_codes[:, g, m].bitcast(FP8X4), lhsT_scale=wo_planes[:, g, m],
+                        rhs=h_codes[:].bitcast(FP8X4), rhs_scale=h_planes[:], start=True, stop=True,
+                    )
+                for e in range(2):
+                    t = 2 * pair + e
+                    nc.scalar.activation(y[:, t, :], logits[:, e, :], ACT.Identity, bias=bo_sb[:, g, t : t + 1])
+            nc.sync.dma_start(out_rows[g][:, :, cols], y[:])
 
         def result_planes(w):
-            width = STRIPS[w] * CHUNK
-            cols = slice(FIRST[w] * CHUNK, FIRST[w] * CHUNK + width)
-            y_codes = held([P, GROUPS, width], I32, "y_codes%d" % w)
+            cols = slice(w * STRIP, (w + 1) * STRIP)
+            y_codes = held([P, GROUPS, STRIP], I32, "y_codes%d" % w)
             for g in range(GROUPS):
-                y_bf = ring.tile([P, width, 4], BF16, name="y_bf", align_bytes=64, bufs=3)
+                k = GROUPS * w + g
+                y_bf = held([P, STRIP, 4], BF16, "y_bf%d" % k, ROUND_BEHIND.get(k))
                 dst = y_bf[:].rearrange("p (c i) t -> p c t i", i=2)
                 src = ys[w, g][:].rearrange("p t (c i) -> p c t i", i=2)
-                if GROUPS * w + g in Y_ON_SCALAR:
+                if k in ROUND_ON_SCALAR:
                     nc.scalar.copy(dst, src)
                 else:
                     nc.vector.tensor_copy(dst, src)
                 nc.vector.quantize_mx(
                     y_codes[:, g, :].bitcast(FP8X4), y_planes[:, g, cols], y_bf[:].rearrange("p n t -> p (n t)")
                 )
-                if w == len(STRIPS) - 1:
+                if w == STRIPS - 1:
                     nc.sync.dma_start(out_words[:, g, cols], y_codes[:, g, :])
-            if w < len(STRIPS) - 1:
+            if w < STRIPS - 1:
                 nc.sync.dma_start(out_words[:, :, cols], y_codes[:])
 
-        wides = len(STRIPS)
-        for w in range(wides + 2):
-            if w < wides:
-                h_bf = ring.tile([P, STRIPS[w], 4 * CHUNK], BF16, name="h_bf", align_bytes=64, bufs=2)
-                larger = ring.tile([P, STRIPS[w], 4 * CHUNK], F32, name="larger", bufs=2)
-                for v in range(STRIPS[w]):
-                    c = FIRST[w] + v
-                    first_stage(c, larger[:, v, :])
-                    if w not in WHOLE_GAIN:
-                        engine = nc.vector if c in GAIN_ON_VECTOR else nc.gpsimd
-                        engine.tensor_tensor(h_bf[:, v, :], larger[:, v, :], gain_sb[:], ALU.mult)
-                if w in WHOLE_GAIN:
-                    nc.vector.tensor_tensor(
-                        h_bf[:], larger[:], gain_sb[:].unsqueeze(1).to_broadcast([P, STRIPS[w], 4 * CHUNK]), ALU.mult
-                    )
-                quantize_h(w, h_bf)
-                for v in range(STRIPS[w]):
-                    c = FIRST[w] + v
-                    if c == 1:
-                        gather(2, 1, 1, 1, "success%d" % c)
-            if w == 0:
-                quantize_wo(0)
-            if 0 <= w - 1 < wides:
-                second_stage(w - 1)
-            if 0 <= w - 2 < wides:
-                result_planes(w - 2)
+        quantize_wo(0)
+        for w in range(2):
+            for u in range(2):
+                difference(w, u)
+        make_h(0)
+        gather(2, 1, 1, 1, "success01")
+        make_h(1)
+        quantize_wo(1)
+        for w in range(STRIPS + 1):
+            if w + 2 < STRIPS:
+                for u in range(2):
+                    difference(w + 2, u)
+                make_h(w + 2)
+            if w < STRIPS:
+                for g in range(GROUPS):
+                    second_stage(w, g)
+            if w >= 1:
+                result_planes(w - 1)
 
         for r in range(4):
             (nc.sync, nc.scalar)[r % 2].dma_start(

@@ -23,10 +23,8 @@ HALF = 512
 ROW0 = 96
 STRIP = 256
 STRIPS = S // STRIP
-CHUNK = 128
-ROUND_ON_SCALAR = (6,)
-ROUND_BEHIND = {0: "success31", 1: "h_bf2", 2: "success30", 3: "h_bf3"}
-GAIN_ON_VECTOR = ()
+ROUND_ON_SCALAR = (0, 1, 2, 6)
+ROUND_BEHIND = {3: "h_bf3", 4: "success31"}
 LOGIT_BANKS = (0, 1, 0, 1, 2, 3, 4, 5, 0, 1, 6, 7, 2, 3, 4, 5)
 
 
@@ -53,7 +51,7 @@ def tile_list_guess_floor_mastery_kernel(
         picked = held([P, 3, S], U8, "picked")
         wq_raw = held([P, PASSES, H // 2], I32, "wq_raw")
         wg_raw = held([P, PASSES, H], I32, "wg_raw")
-        gain_sb = held([P, CHUNK * 4], F32, "gain_sb")
+        gain_sb = held([P, STRIP * 4], F32, "gain_sb")
         gain_raw = held([P, 4, 8], F32, "gain_raw")
         bo_sb = held([P, GROUPS, 4], F32, "bo_sb")
 
@@ -168,7 +166,7 @@ def tile_list_guess_floor_mastery_kernel(
             for l in range(3 - h):
                 gather(l, 1, h, 1)
         nc.gpsimd.tensor_copy(
-            gain_sb[:].rearrange("p (n t) -> p n t", t=4), gain_raw[:, :, 0].unsqueeze(1).to_broadcast([P, CHUNK, 4])
+            gain_sb[:].rearrange("p (n t) -> p n t", t=4), gain_raw[:, :, 0].unsqueeze(1).to_broadcast([P, STRIP, 4])
         )
 
         wo_codes = held([P, GROUPS, 512], U32, "wo_codes")
@@ -232,20 +230,17 @@ def tile_list_guess_floor_mastery_kernel(
         h_mx = {}
 
         def make_h(w):
-            larger = held([P, 2, STRIP, 2], F32, "larger%d" % w, "h_bf%d" % (w - 2) if w >= 2 else None)
+            larger = held([P, 2, STRIP, 2], F32, "larger%d" % w, ("wa_raw%d", "wa_bf%d")[w // 2] % (w % 2))
             for u in range(2):
                 guess_floor(w, u, larger)
-            h_bf = held([P, STRIP // CHUNK, CHUNK, 2, 2], BF16, "h_bf%d" % w)
-            for c in range(STRIP // CHUNK):
-                (nc.vector if (w, c) in GAIN_ON_VECTOR else nc.gpsimd).tensor_tensor(
-                    h_bf[:, c],
-                    larger[:, :, CHUNK * c : CHUNK * (c + 1), :].rearrange("p u n i -> p n u i"),
-                    gain_sb[:].rearrange("p (n u i) -> p n u i", u=2, i=2),
-                    ALU.mult,
-                )
+            h_bf = held([P, STRIP, 2, 2], BF16, "h_bf%d" % w)
+            nc.vector.tensor_tensor(
+                h_bf[:], larger[:].rearrange("p u n i -> p n u i"),
+                gain_sb[:].rearrange("p (n u i) -> p n u i", u=2, i=2), ALU.mult,
+            )
             h_codes = held([P, STRIP], U32, "h_codes%d" % w)
             h_planes = held([P, STRIP], U8, "h_planes%d" % w)
-            nc.vector.quantize_mx(h_codes[:].bitcast(FP8X4), h_planes[:], h_bf[:].rearrange("p c n u i -> p (c n u i)"))
+            nc.vector.quantize_mx(h_codes[:].bitcast(FP8X4), h_planes[:], h_bf[:].rearrange("p n u i -> p (n u i)"))
             h_mx[w] = (h_codes, h_planes)
 
         ys = {}

@@ -23,8 +23,9 @@ HALF = 512
 ROW0 = 96
 STRIP = 256
 STRIPS = S // STRIP
-ROUND_ON_SCALAR = (0, 1, 2, 6)
-ROUND_BEHIND = {3: "h_bf3", 4: "success31"}
+CHUNK = 128
+ROUND_ON_SCALAR = (0, 6)
+ROUND_BEHIND = {1: "h_bf", 2: "larger0", 3: "wo_bf1"}
 LOGIT_BANKS = (0, 1, 0, 1, 2, 3, 4, 5, 0, 1, 6, 7, 2, 3, 4, 5)
 
 
@@ -51,7 +52,7 @@ def tile_list_guess_floor_mastery_kernel(
         picked = held([P, 3, S], U8, "picked")
         wq_raw = held([P, PASSES, H // 2], I32, "wq_raw")
         wg_raw = held([P, PASSES, H], I32, "wg_raw")
-        gain_sb = held([P, STRIP * 4], F32, "gain_sb")
+        gain_sb = held([P, CHUNK * 4], F32, "gain_sb")
         gain_raw = held([P, 4, 8], F32, "gain_raw")
         bo_sb = held([P, GROUPS, 4], F32, "bo_sb")
 
@@ -166,10 +167,10 @@ def tile_list_guess_floor_mastery_kernel(
             for l in range(3 - h):
                 gather(l, 1, h, 1)
         nc.gpsimd.tensor_copy(
-            gain_sb[:].rearrange("p (n t) -> p n t", t=4), gain_raw[:, :, 0].unsqueeze(1).to_broadcast([P, STRIP, 4])
+            gain_sb[:].rearrange("p (n t) -> p n t", t=4), gain_raw[:, :, 0].unsqueeze(1).to_broadcast([P, CHUNK, 4])
         )
 
-        wo_codes = held([P, GROUPS, 512], U32, "wo_codes")
+        wo_codes = {}
         wo_planes = held([P, GROUPS, 512], U8, "wo_planes")
 
         def quantize_wo(g):
@@ -179,10 +180,12 @@ def tile_list_guess_floor_mastery_kernel(
             for m in range(0, 128, 64):
                 for u in range(2):
                     nc.scalar.copy(dst[:, u, m : m + 64], src[:, u, m : m + 64])
+            wo_codes[g] = held([P, 512], U32, "wo_codes%d" % g, (None, "larger1")[g])
             nc.vector.quantize_mx(
-                wo_codes[:, g, :].bitcast(FP8X4), wo_planes[:, g, :], wo_bf[:].rearrange("p t m j -> p (t m j)")
+                wo_codes[g][:].bitcast(FP8X4), wo_planes[:, g, :], wo_bf[:].rearrange("p t m j -> p (t m j)")
             )
 
+        y_codes = held([P, GROUPS, S], I32, "y_codes")
         y_planes = held([P, GROUPS, S], U8, "y_planes")
         out_rows = out_0.rearrange("(g p t) j -> g p t j", g=GROUPS, t=4)
         out_words = out_1.rearrange("g p m i -> p g (m i)").bitcast(I32)
@@ -227,20 +230,29 @@ def tile_list_guess_floor_mastery_kernel(
                     )
             nc.vector.tensor_tensor(larger[:, u], guess[:].rearrange("p i n -> p n i"), success[w, u][:], ALU.max)
 
-        h_mx = {}
+        larger, h_bf, h_mx = {}, {}, {}
 
-        def make_h(w):
-            larger = held([P, 2, STRIP, 2], F32, "larger%d" % w, ("wa_raw%d", "wa_bf%d")[w // 2] % (w % 2))
+        def maxima(w):
+            larger[w] = held([P, 2, STRIP, 2], F32, "larger%d" % w, ("larger0", "larger1", "larger0", "wo_bf1")[w])
             for u in range(2):
-                guess_floor(w, u, larger)
-            h_bf = held([P, STRIP, 2, 2], BF16, "h_bf%d" % w)
-            nc.vector.tensor_tensor(
-                h_bf[:], larger[:].rearrange("p u n i -> p n u i"),
-                gain_sb[:].rearrange("p (n u i) -> p n u i", u=2, i=2), ALU.mult,
+                guess_floor(w, u, larger[w])
+
+        def times_gain(w, c, engine):
+            if w not in h_bf:
+                h_bf[w] = held([P, STRIP // CHUNK, CHUNK, 2, 2], BF16, "h_bf%d" % w, "h_bf")
+            engine.tensor_tensor(
+                h_bf[w][:, c],
+                larger[w][:, :, CHUNK * c : CHUNK * (c + 1), :].rearrange("p u n i -> p n u i"),
+                gain_sb[:].rearrange("p (n u i) -> p n u i", u=2, i=2),
+                ALU.mult,
             )
+
+        def quantize_h(w):
             h_codes = held([P, STRIP], U32, "h_codes%d" % w)
             h_planes = held([P, STRIP], U8, "h_planes%d" % w)
-            nc.vector.quantize_mx(h_codes[:].bitcast(FP8X4), h_planes[:], h_bf[:].rearrange("p n u i -> p (n u i)"))
+            nc.vector.quantize_mx(
+                h_codes[:].bitcast(FP8X4), h_planes[:], h_bf[w][:].rearrange("p c n u i -> p (c n u i)")
+            )
             h_mx[w] = (h_codes, h_planes)
 
         ys = {}
@@ -256,7 +268,7 @@ def tile_list_guess_floor_mastery_kernel(
                 for e in range(2):
                     m = slice(128 * (2 * pair + e), 128 * (2 * pair + e + 1))
                     nc.tensor.matmul_mx(
-                        logits[:, e, :], lhsT=wo_codes[:, g, m].bitcast(FP8X4), lhsT_scale=wo_planes[:, g, m],
+                        logits[:, e, :], lhsT=wo_codes[g][:, m].bitcast(FP8X4), lhsT_scale=wo_planes[:, g, m],
                         rhs=h_codes[:].bitcast(FP8X4), rhs_scale=h_planes[:], start=True, stop=True,
                     )
                 for e in range(2):
@@ -266,7 +278,6 @@ def tile_list_guess_floor_mastery_kernel(
 
         def result_planes(w):
             cols = slice(w * STRIP, (w + 1) * STRIP)
-            y_codes = held([P, GROUPS, STRIP], I32, "y_codes%d" % w)
             for g in range(GROUPS):
                 k = GROUPS * w + g
                 y_bf = held([P, STRIP, 4], BF16, "y_bf%d" % k, ROUND_BEHIND.get(k))
@@ -277,31 +288,42 @@ def tile_list_guess_floor_mastery_kernel(
                 else:
                     nc.vector.tensor_copy(dst, src)
                 nc.vector.quantize_mx(
-                    y_codes[:, g, :].bitcast(FP8X4), y_planes[:, g, cols], y_bf[:].rearrange("p n t -> p (n t)")
+                    y_codes[:, g, cols].bitcast(FP8X4), y_planes[:, g, cols], y_bf[:].rearrange("p n t -> p (n t)")
                 )
                 if w == STRIPS - 1:
-                    nc.sync.dma_start(out_words[:, g, cols], y_codes[:, g, :])
-            if w < STRIPS - 1:
-                nc.sync.dma_start(out_words[:, :, cols], y_codes[:])
+                    nc.sync.dma_start(out_words[:, g, cols], y_codes[:, g, cols])
+            if w == STRIPS - 2:
+                nc.sync.dma_start(out_words[:, :, : S - STRIP], y_codes[:, :, : S - STRIP])
 
         quantize_wo(0)
         for w in range(2):
             for u in range(2):
                 difference(w, u)
-        make_h(0)
+        maxima(0)
+        for c in range(2):
+            times_gain(0, c, nc.gpsimd)
         gather(2, 1, 1, 1, "success01")
-        make_h(1)
-        quantize_wo(1)
-        for w in range(STRIPS + 1):
+        maxima(1)
+        quantize_h(0)
+        for w in range(1, STRIPS - 1):
+            times_gain(w, 0, nc.gpsimd)
+            for u in range(2):
+                difference(w + 1, u)
+            maxima(w + 1)
+            times_gain(w, 1, nc.vector)
+            if w == 1:
+                quantize_wo(1)
+            quantize_h(w)
+            for g in range(GROUPS):
+                second_stage(w - 1, g)
+        for c in range(2):
+            times_gain(STRIPS - 1, c, nc.vector)
+        quantize_h(STRIPS - 1)
+        for w in range(STRIPS):
             if w + 2 < STRIPS:
-                for u in range(2):
-                    difference(w + 2, u)
-                make_h(w + 2)
-            if w < STRIPS:
                 for g in range(GROUPS):
-                    second_stage(w, g)
-            if w >= 1:
-                result_planes(w - 1)
+                    second_stage(w + 2, g)
+            result_planes(w)
 
         for r in range(4):
             (nc.sync, nc.scalar)[r % 2].dma_start(

@@ -26,6 +26,7 @@ STRIPS = S // STRIP
 CHUNK = 128
 ROUND_ON_SCALAR = (0, 6)
 ROUND_BEHIND = {1: "h_bf", 2: "larger0", 3: "wo_bf1"}
+Y_ORDER = [(0, 0), (0, 1), (1, 0), (1, 1), (2, 0), (3, 0), (2, 1), (3, 1)]
 LOGIT_BANKS = (0, 1, 0, 1, 2, 3, 4, 5, 0, 1, 6, 7, 2, 3, 4, 5)
 
 
@@ -258,13 +259,15 @@ def tile_list_guess_floor_mastery_kernel(
         ys = {}
 
         def second_stage(w, g):
-            cols = slice(w * STRIP, (w + 1) * STRIP)
+            h, v = divmod(w, HALF // STRIP)
+            cols = slice(v * STRIP, (v + 1) * STRIP)
             h_codes, h_planes = h_mx[w]
-            y = held([P, 4, STRIP], F32, "y%d%d" % (w, g))
-            ys[w, g] = y
+            if (h, g) not in ys:
+                ys[h, g] = held([P, 4, HALF], F32, "y%d%d" % (h, g))
+            y = ys[h, g]
             for pair in range(2):
-                j = 2 * (GROUPS * w + g) + pair
-                logits = psum.tile([P, 2, STRIP], F32, name="logits", tag="bank%d" % LOGIT_BANKS[j])
+                bank = LOGIT_BANKS[2 * Y_ORDER.index((w, g)) + pair]
+                logits = psum.tile([P, 2, STRIP], F32, name="logits", tag="bank%d" % bank)
                 for e in range(2):
                     m = slice(128 * (2 * pair + e), 128 * (2 * pair + e + 1))
                     nc.tensor.matmul_mx(
@@ -273,27 +276,29 @@ def tile_list_guess_floor_mastery_kernel(
                     )
                 for e in range(2):
                     t = 2 * pair + e
-                    nc.scalar.activation(y[:, t, :], logits[:, e, :], ACT.Identity, bias=bo_sb[:, g, t : t + 1])
-            nc.sync.dma_start(out_rows[g][:, :, cols], y[:])
+                    nc.scalar.activation(y[:, t, cols], logits[:, e, :], ACT.Identity, bias=bo_sb[:, g, t : t + 1])
+                if v == 1:
+                    slots = slice(2 * pair, 2 * pair + 2)
+                    nc.sync.dma_start(out_rows[g][:, slots, HALF * h : HALF * (h + 1)], y[:, slots, :])
 
-        def result_planes(w):
+        def result_planes(w, g):
+            h, v = divmod(w, HALF // STRIP)
+            k = Y_ORDER.index((w, g))
             cols = slice(w * STRIP, (w + 1) * STRIP)
-            for g in range(GROUPS):
-                k = GROUPS * w + g
-                y_bf = held([P, STRIP, 4], BF16, "y_bf%d" % k, ROUND_BEHIND.get(k))
-                dst = y_bf[:].rearrange("p (c i) t -> p c t i", i=2)
-                src = ys[w, g][:].rearrange("p t (c i) -> p c t i", i=2)
-                if k in ROUND_ON_SCALAR:
-                    nc.scalar.copy(dst, src)
-                else:
-                    nc.vector.tensor_copy(dst, src)
-                nc.vector.quantize_mx(
-                    y_codes[:, g, cols].bitcast(FP8X4), y_planes[:, g, cols], y_bf[:].rearrange("p n t -> p (n t)")
-                )
-                if w == STRIPS - 1:
-                    nc.sync.dma_start(out_words[:, g, cols], y_codes[:, g, cols])
-            if w == STRIPS - 2:
-                nc.sync.dma_start(out_words[:, :, : S - STRIP], y_codes[:, :, : S - STRIP])
+            y_bf = held([P, STRIP, 4], BF16, "y_bf%d" % k, ROUND_BEHIND.get(k))
+            dst = y_bf[:].rearrange("p (c i) t -> p c t i", i=2)
+            src = ys[h, g][:, :, v * STRIP : (v + 1) * STRIP].rearrange("p t (c i) -> p c t i", i=2)
+            if k in ROUND_ON_SCALAR:
+                nc.scalar.copy(dst, src)
+            else:
+                nc.vector.tensor_copy(dst, src)
+            nc.vector.quantize_mx(
+                y_codes[:, g, cols].bitcast(FP8X4), y_planes[:, g, cols], y_bf[:].rearrange("p n t -> p (n t)")
+            )
+            if (w, g) == (1, 1):
+                nc.sync.dma_start(out_words[:, :, :HALF], y_codes[:, :, :HALF])
+            if w == STRIPS - 1:
+                nc.sync.dma_start(out_words[:, g, HALF:], y_codes[:, g, HALF:])
 
         quantize_wo(0)
         for w in range(2):
@@ -319,11 +324,10 @@ def tile_list_guess_floor_mastery_kernel(
         for c in range(2):
             times_gain(STRIPS - 1, c, nc.vector)
         quantize_h(STRIPS - 1)
-        for w in range(STRIPS):
-            if w + 2 < STRIPS:
-                for g in range(GROUPS):
-                    second_stage(w + 2, g)
-            result_planes(w)
+        for w, g in Y_ORDER[4:]:
+            second_stage(w, g)
+        for w, g in Y_ORDER:
+            result_planes(w, g)
 
         for r in range(4):
             (nc.sync, nc.scalar)[r % 2].dma_start(

@@ -43,10 +43,10 @@ def tile_list_guess_floor_mastery_kernel(
             return keep.tile(shape, dtype, name=name, tag=tag or name, align_bytes=64)
 
         lists = [held([P, S // 16], U16, "list%d" % l) for l in range(3)]
-        tab = [held([P, T], I32, "tab%d" % a) for a in range(PASSES)]
+        tab = [held([P, T], I32, "tab0")]
         tab_rows = held([P, T], U8, "tab_rows")
-        w_rows = held([P, 2, PASSES, H], U8, "w_rows")
-        w_planes = held([P, 2, PASSES, H], U8, "w_planes")
+        w_rows = [held([P, PASSES, H], U8, "w_rows%d" % i) for i in range(2)]
+        w_planes = [held([P, PASSES, H], U8, "w_planes%d" % i) for i in range(2)]
         planes = [[held([P, 3 * HALF], U8, "planes%d%d" % (h, a)) for a in range(PASSES)] for h in range(2)]
         wa_raw = [held([P, 4, H], F32, "wa_raw%d" % a) for a in range(PASSES)]
         wo_raw = [held([P, 4, 512], F32, "wo_raw%d" % g) for g in range(GROUPS)]
@@ -57,7 +57,8 @@ def tile_list_guess_floor_mastery_kernel(
         gain_raw = held([P, 4, 8], F32, "gain_raw")
         bo_sb = held([P, GROUPS, 4], F32, "bo_sb")
 
-        nc.gpsimd.memset(w_rows[:].rearrange("p i a e -> p (i a e)").bitcast(I32), 0)
+        for i in range(2):
+            nc.gpsimd.memset(w_rows[i][:].rearrange("p a e -> p (a e)").bitcast(I32), 0)
         nc.vector.memset(tab_rows[0:ROW0, :].bitcast(I32), 0)
         for h, engine in enumerate((nc.vector, nc.gpsimd)):
             for a in range(PASSES):
@@ -81,7 +82,13 @@ def tile_list_guess_floor_mastery_kernel(
         def load_w_rows(i, r):
             src = (wq_scales, wg_scales)[i]
             nc.sync.dma_start(
-                w_rows[r:P:32, i].bitcast(I32), src[:, r:16:4, :].rearrange("a q e -> q a e").bitcast(I32)
+                w_rows[i][r:P:32].bitcast(I32), src[:, r:16:4, :].rearrange("a q e -> q a e").bitcast(I32)
+            )
+
+        def sort_w_rows(i):
+            nc.gpsimd.tensor_copy(
+                w_planes[i][:].bitcast(I32).rearrange("p a (t b w) -> p a t b w", t=4, w=2),
+                w_rows[i][:].bitcast(I32).rearrange("p a (b t w) -> p a t b w", t=4, w=2),
             )
 
         def move_plane(h, a, r):
@@ -98,37 +105,32 @@ def tile_list_guess_floor_mastery_kernel(
         load_wa(0)
         for r in range(4):
             load_w_rows(0, r)
-        load_w_rows(1, 0)
-        load_w_rows(1, 1)
         load_wa(1)
-        load_w_rows(1, 2)
-        load_w_rows(1, 3)
-        load_tab(1)
         nc.sync.dma_start(wq_raw[:], wq_words.rearrange("a p e -> p a e").bitcast(I32))
 
         for l in range(3):
             nc.vector.tensor_copy(picked[:, l, :], tab_rows[:].indirect(lists[l][:]))
-        nc.gpsimd.tensor_copy(
-            w_planes[:].bitcast(I32).rearrange("p i a (t b w) -> p (i a) t b w", t=4, w=2),
-            w_rows[:].bitcast(I32).rearrange("p i a (b t w) -> p (i a) t b w", t=4, w=2),
-        )
-        nc.sync.dma_start(bo_sb[:], bo.rearrange("(g p t) -> p g t", g=GROUPS, t=4))
+        sort_w_rows(0)
         for r in range(4):
             move_plane(0, 0, r)
-        load_wo(0, 0)
-        load_wo(0, 1)
+        tab.append(held([P, T], I32, "tab1", "tab_rows"))
+        load_tab(1)
         for r in range(4):
             move_plane(0, 1, r)
-        load_wo(0, 2)
-        load_wo(0, 3)
         nc.sync.dma_start(wg_raw[:], wg_words.rearrange("a p e i -> p a (e i)").bitcast(I32))
+        for r in range(4):
+            load_w_rows(1, r)
+        sort_w_rows(1)
+        nc.sync.dma_start(bo_sb[:], bo.rearrange("(g p t) -> p g t", g=GROUPS, t=4))
+        for t in range(4):
+            load_wo(0, t)
         for t in range(4):
             load_gain(t)
-        for t in range(4):
-            load_wo(1, t)
         for a in range(PASSES):
             for r in range(4):
-                move_plane(1, a, r)
+                move_plane(1, 1 - a, r)
+            for t in range(2):
+                load_wo(1, 2 * a + t)
 
         words = {}
 
@@ -139,7 +141,7 @@ def tile_list_guess_floor_mastery_kernel(
             for i in range(count):
                 words[l, a, first + i] = room[:, i * HALF : (i + 1) * HALF]
 
-        for l in range(3):
+        for l in range(2):
             gather(l, 0, 0, 2)
 
         wa_codes = held([P, PASSES, H], U32, "wa_codes")
@@ -152,6 +154,8 @@ def tile_list_guess_floor_mastery_kernel(
             nc.vector.quantize_mx(
                 wa_codes[:, a, :].bitcast(FP8X4), wa_planes[:, a, :], wa_bf[:].rearrange("p t b q j -> p (t b q j)")
             )
+            if a == 0:
+                gather(2, 0, 0, 2, "wa_bf0")
 
         wq_codes = held([P, PASSES, 2 * H], U8, "wq_codes")
         wg_codes = [held([P, PASSES, H // 2], I32, "wg_codes%d" % u) for u in range(2)]
@@ -212,7 +216,7 @@ def tile_list_guess_floor_mastery_kernel(
                     t = 2 * u + i
                     nc.tensor.matmul_mx(
                         diff[:, i, :], lhsT=wq_codes[:, a, 256 * t : 256 * (t + 1)].bitcast(FP4X4),
-                        lhsT_scale=w_planes[:, 0, a, 128 * t : 128 * (t + 1)],
+                        lhsT_scale=w_planes[0][:, a, 128 * t : 128 * (t + 1)],
                         rhs=moving(1, a, w)[0], rhs_scale=moving(1, a, w)[1],
                         start=False, stop=(a == PASSES - 1 and i == 1),
                     )
@@ -225,7 +229,7 @@ def tile_list_guess_floor_mastery_kernel(
                 for i in range(2):
                     m = slice(128 * (2 * u + i), 128 * (2 * u + i + 1))
                     nc.tensor.matmul_mx(
-                        guess[:, i, :], lhsT=wg_codes[u][:, a, 128 * i : 128 * (i + 1)].bitcast(FP8X4), lhsT_scale=w_planes[:, 1, a, m],
+                        guess[:, i, :], lhsT=wg_codes[u][:, a, 128 * i : 128 * (i + 1)].bitcast(FP8X4), lhsT_scale=w_planes[1][:, a, m],
                         rhs=moving(2, a, w)[0], rhs_scale=moving(2, a, w)[1],
                         start=(a == 0 and i == 0), stop=(a == PASSES - 1 and i == 1),
                     )
@@ -300,7 +304,6 @@ def tile_list_guess_floor_mastery_kernel(
             if w == STRIPS - 1:
                 nc.sync.dma_start(out_words[:, g, HALF:], y_codes[:, g, HALF:])
 
-        quantize_wo(0)
         for w in range(2):
             for u in range(2):
                 difference(w, u)
@@ -309,6 +312,7 @@ def tile_list_guess_floor_mastery_kernel(
             times_gain(0, c, nc.gpsimd)
         gather(2, 1, 1, 1, "success01")
         maxima(1)
+        quantize_wo(0)
         quantize_h(0)
         for w in range(1, STRIPS - 1):
             times_gain(w, 0, nc.gpsimd)

@@ -54,7 +54,7 @@ def tile_list_guess_floor_mastery_kernel(
         wq_raw = held([P, PASSES, H // 2], I32, "wq_raw")
         wg_raw = held([P, PASSES, H], I32, "wg_raw")
         gain_sb = held([P, CHUNK * 4], F32, "gain_sb")
-        gain_raw = held([P, 4, 8], F32, "gain_raw")
+        gain_raw = held([P, 4], F32, "gain_raw")
         bo_sb = held([P, GROUPS, 4], F32, "bo_sb")
 
         for i in range(2):
@@ -70,14 +70,8 @@ def tile_list_guess_floor_mastery_kernel(
         def load_wa(a):
             nc.sync.dma_start(wa_raw[a][:], wa[512 * a : 512 * (a + 1), :].rearrange("(p j) r -> p j r", j=4))
 
-        def load_gain(t):
-            with nc.allow_non_contiguous_dma(reason="one gain to each partition and slot"):
-                nc.sync.dma_start(gain_raw[:, t, 0:1], gain.rearrange("(b t q) -> t b q", t=4, q=8)[t].unsqueeze(2))
-
-        wo_rows = wo.rearrange("(b t q) n -> t b q n", t=4, q=8)
-
-        def load_wo(g, t):
-            nc.sync.dma_start(wo_raw[g][:, t, :], wo_rows[t][:, :, 512 * g : 512 * (g + 1)])
+        def load_wo(g):
+            nc.sync.dma_start(wo_raw[g][:], wo[:, 512 * g : 512 * (g + 1)].rearrange("(p j) n -> p j n", j=4))
 
         def load_w_rows(i, r):
             src = (wq_scales, wg_scales)[i]
@@ -87,8 +81,8 @@ def tile_list_guess_floor_mastery_kernel(
 
         def sort_w_rows(i):
             nc.gpsimd.tensor_copy(
-                w_planes[i][:].bitcast(I32).rearrange("p a (t b w) -> p a t b w", t=4, w=2),
-                w_rows[i][:].bitcast(I32).rearrange("p a (b t w) -> p a t b w", t=4, w=2),
+                w_planes[i][:].rearrange("p a (t m) -> p a t m", t=4),
+                w_rows[i][:].rearrange("p a (m t) -> p a t m", t=4),
             )
 
         def move_plane(h, a, r):
@@ -105,8 +99,8 @@ def tile_list_guess_floor_mastery_kernel(
         load_wa(0)
         for r in range(4):
             load_w_rows(0, r)
-        load_wa(1)
         nc.sync.dma_start(wq_raw[:], wq_words.rearrange("a p e -> p a e").bitcast(I32))
+        load_wa(1)
 
         for l in range(3):
             nc.vector.tensor_copy(picked[:, l, :], tab_rows[:].indirect(lists[l][:]))
@@ -122,15 +116,13 @@ def tile_list_guess_floor_mastery_kernel(
             load_w_rows(1, r)
         sort_w_rows(1)
         nc.sync.dma_start(bo_sb[:], bo.rearrange("(g p t) -> p g t", g=GROUPS, t=4))
-        for t in range(4):
-            load_wo(0, t)
-        for t in range(4):
-            load_gain(t)
-        for a in range(PASSES):
-            for r in range(4):
-                move_plane(1, 1 - a, r)
-            for t in range(2):
-                load_wo(1, 2 * a + t)
+        load_wo(0)
+        nc.sync.dma_start(gain_raw[:], gain.rearrange("(p t) -> p t", t=4))
+        for r in range(4):
+            move_plane(1, 1, r)
+        load_wo(1)
+        for r in range(4):
+            move_plane(1, 0, r)
 
         words = {}
 
@@ -147,32 +139,33 @@ def tile_list_guess_floor_mastery_kernel(
         wa_codes = held([P, PASSES, H], U32, "wa_codes")
         wa_planes = held([P, PASSES, H], U8, "wa_planes")
         for a in range(PASSES):
-            wa_bf = held([P, 4, 16, 8, 4], BF16, "wa_bf%d" % a)
-            src = wa_raw[a][:].rearrange("p j (b t q) -> p t b q j", t=4, q=8)
-            for t in range(4):
-                nc.scalar.activation(wa_bf[:, t], src[:, t], ACT.Copy, scale=-1.0)
+            wa_bf = held([P, 4, 128, 4], BF16, "wa_bf%d" % a)
+            dst = wa_bf[:].rearrange("p (u i) m j -> p u m j i", i=2)
+            src = wa_raw[a][:].rearrange("p j (m u i) -> p u m j i", u=2, i=2)
+            for u in range(2):
+                nc.scalar.activation(dst[:, u], src[:, u], ACT.Copy, scale=-1.0)
             nc.vector.quantize_mx(
-                wa_codes[:, a, :].bitcast(FP8X4), wa_planes[:, a, :], wa_bf[:].rearrange("p t b q j -> p (t b q j)")
+                wa_codes[:, a, :].bitcast(FP8X4), wa_planes[:, a, :], wa_bf[:].rearrange("p t m j -> p (t m j)")
             )
             if a == 0:
                 gather(2, 0, 0, 2, "wa_bf0")
 
         wq_codes = held([P, PASSES, 2 * H], U8, "wq_codes")
         wg_codes = [held([P, PASSES, H // 2], I32, "wg_codes%d" % u) for u in range(2)]
-        nc.gpsimd.tensor_copy(
-            wq_codes[:].bitcast(I32).rearrange("p a (t b w) -> p a t b w", t=4, w=4),
-            wq_raw[:].rearrange("p a (b t w) -> p a t b w", t=4, w=4),
+        nc.scalar.copy(
+            wq_codes[:].bitcast(U16).rearrange("p a (u i m) -> p a u m i", u=2, i=2),
+            wq_raw[:].bitcast(U16).rearrange("p a (m u i) -> p a u m i", u=2, i=2),
         )
         for u in range(2):
             nc.gpsimd.tensor_copy(
-                wg_codes[u][:].rearrange("p a (i b w) -> p a i b w", i=2, w=8),
-                wg_raw[:].rearrange("p a (b t w) -> p a t b w", t=4, w=8)[:, :, 2 * u : 2 * u + 2],
+                wg_codes[u][:].rearrange("p a (i m) -> p a i m", i=2),
+                wg_raw[:].rearrange("p a (m t) -> p a t m", t=4)[:, :, 2 * u : 2 * u + 2],
             )
         for h in range(2):
             for l in range(3 - h):
                 gather(l, 1, h, 1)
         nc.gpsimd.tensor_copy(
-            gain_sb[:].rearrange("p (n t) -> p n t", t=4), gain_raw[:, :, 0].unsqueeze(1).to_broadcast([P, CHUNK, 4])
+            gain_sb[:].rearrange("p (n t) -> p n t", t=4), gain_raw[:].unsqueeze(1).to_broadcast([P, CHUNK, 4])
         )
 
         wo_codes = {}

@@ -24,9 +24,8 @@ ROW0 = 96
 STRIP = 256
 STRIPS = S // STRIP
 CHUNK = 128
-ROUND_ON_SCALAR = (0, 6)
-ROUND_BEHIND = {1: "h_bf", 2: "larger0", 3: "wo_bf1"}
-Y_ORDER = [(0, 0), (0, 1), (1, 0), (1, 1), (2, 0), (3, 0), (2, 1), (3, 1)]
+ROUND_BEHIND = {(0, 0): "wo_bf1", (0, 1): "h_bf"}
+Y_ORDER = [(0, 0), (0, 1), (1, 0), (1, 1), (2, 0), (2, 1), (3, 0), (3, 1)]
 LOGIT_BANKS = (0, 1, 0, 1, 2, 3, 4, 5, 0, 1, 6, 7, 2, 3, 4, 5)
 
 
@@ -274,28 +273,26 @@ def tile_list_guess_floor_mastery_kernel(
                 for e in range(2):
                     t = 2 * pair + e
                     nc.scalar.activation(y[:, t, cols], logits[:, e, :], ACT.Identity, bias=bo_sb[:, g, t : t + 1])
-                if v == 1:
-                    slots = slice(2 * pair, 2 * pair + 2)
-                    nc.sync.dma_start(out_rows[g][:, slots, HALF * h : HALF * (h + 1)], y[:, slots, :])
+            nc.sync.dma_start(out_rows[g][:, :, w * STRIP : (w + 1) * STRIP], y[:, :, cols])
 
-        def result_planes(w, g):
-            h, v = divmod(w, HALF // STRIP)
-            k = Y_ORDER.index((w, g))
-            cols = slice(w * STRIP, (w + 1) * STRIP)
-            y_bf = held([P, STRIP, 4], BF16, "y_bf%d" % k, ROUND_BEHIND.get(k))
-            dst = y_bf[:].rearrange("p (c i) t -> p c t i", i=2)
-            src = ys[h, g][:, :, v * STRIP : (v + 1) * STRIP].rearrange("p t (c i) -> p c t i", i=2)
-            if k in ROUND_ON_SCALAR:
-                nc.scalar.copy(dst, src)
-            else:
-                nc.vector.tensor_copy(dst, src)
-            nc.vector.quantize_mx(
-                y_codes[:, g, cols].bitcast(FP8X4), y_planes[:, g, cols], y_bf[:].rearrange("p n t -> p (n t)")
+        y_bf = {}
+
+        def round_y(engine_copy, h, g, first, count):
+            if (h, g) not in y_bf:
+                y_bf[h, g] = held([P, HALF, 4], BF16, "y_bf%d%d" % (h, g), ROUND_BEHIND.get((h, g)))
+            cols = slice(first * STRIP, (first + count) * STRIP)
+            engine_copy(
+                y_bf[h, g][:, cols].rearrange("p (c i) t -> p c t i", i=2),
+                ys[h, g][:, :, cols].rearrange("p t (c i) -> p c t i", i=2),
             )
-            if (w, g) == (1, 1):
-                nc.sync.dma_start(out_words[:, :, :HALF], y_codes[:, :, :HALF])
-            if w == STRIPS - 1:
-                nc.sync.dma_start(out_words[:, g, HALF:], y_codes[:, g, HALF:])
+
+        def quantize_y(h, g, first, count):
+            cols = slice(first * STRIP, (first + count) * STRIP)
+            out_cols = slice(h * HALF + first * STRIP, h * HALF + (first + count) * STRIP)
+            nc.vector.quantize_mx(
+                y_codes[:, g, out_cols].bitcast(FP8X4), y_planes[:, g, out_cols],
+                y_bf[h, g][:, cols].rearrange("p n t -> p (n t)"),
+            )
 
         for w in range(2):
             for u in range(2):
@@ -323,8 +320,20 @@ def tile_list_guess_floor_mastery_kernel(
         quantize_h(STRIPS - 1)
         for w, g in Y_ORDER[4:]:
             second_stage(w, g)
-        for w, g in Y_ORDER:
-            result_planes(w, g)
+        for g in range(GROUPS):
+            round_y(nc.vector.tensor_copy, 0, g, 0, 2)
+        for g in range(GROUPS):
+            quantize_y(0, g, 0, 2)
+        nc.sync.dma_start(out_words[:, :, :HALF], y_codes[:, :, :HALF])
+        round_y(nc.vector.tensor_copy, 1, 0, 0, 2)
+        quantize_y(1, 0, 0, 2)
+        nc.sync.dma_start(out_words[:, 0, HALF:], y_codes[:, 0, HALF:])
+        round_y(nc.scalar.copy, 1, 1, 0, 1)
+        round_y(nc.vector.tensor_copy, 1, 1, 1, 1)
+        for v in (1, 0):
+            quantize_y(1, 1, v, 1)
+            cols = slice(HALF + v * STRIP, HALF + (v + 1) * STRIP)
+            nc.sync.dma_start(out_words[:, 1, cols], y_codes[:, 1, cols])
 
         for r in range(4):
             (nc.sync, nc.scalar)[r % 2].dma_start(

@@ -46,7 +46,10 @@ def tile_list_guess_floor_mastery_kernel(
         tab_rows = held([P, T], U8, "tab_rows")
         w_rows = [held([P, PASSES, H], U8, "w_rows%d" % i) for i in range(2)]
         w_planes = [held([P, PASSES, H], U8, "w_planes%d" % i) for i in range(2)]
-        planes = [[held([P, 3 * HALF], U8, "planes%d%d" % (h, a)) for a in range(PASSES)] for h in range(2)]
+        planes = {
+            (a, first): held([P, 3, count * HALF], U8, "planes%d%d" % (a, first))
+            for a, first, count in ((0, 0, 2), (1, 0, 1), (1, 1, 1))
+        }
         wa_raw = [held([P, 4, H], F32, "wa_raw%d" % a) for a in range(PASSES)]
         wo_raw = [held([P, 4, 512], F32, "wo_raw%d" % g) for g in range(GROUPS)]
         picked = held([P, 3, S], U8, "picked")
@@ -59,9 +62,8 @@ def tile_list_guess_floor_mastery_kernel(
         for i in range(2):
             nc.gpsimd.memset(w_rows[i][:].rearrange("p a e -> p (a e)").bitcast(I32), 0)
         nc.vector.memset(tab_rows[0:ROW0, :].bitcast(I32), 0)
-        for h, engine in enumerate((nc.vector, nc.gpsimd)):
-            for a in range(PASSES):
-                engine.memset(planes[h][a][:].bitcast(I32), 0)
+        for (a, first), plane in planes.items():
+            (nc.vector, nc.gpsimd)[a].memset(plane[:].rearrange("p l e -> p (l e)").bitcast(I32), 0)
 
         def load_tab(a):
             nc.sync.dma_start(tab[a][:], tab_words[a].rearrange("p t i -> p (t i)").bitcast(I32))
@@ -84,11 +86,10 @@ def tile_list_guess_floor_mastery_kernel(
                 w_rows[i][:].rearrange("p a (m t) -> p a t m", t=4),
             )
 
-        def move_plane(h, a, r):
+        def move_plane(a, first, count, r):
             rows = slice(ROW0 + 16 * a + r, ROW0 + 16 * (a + 1), 4)
             nc.sync.dma_start(
-                planes[h][a][r:P:32, :].bitcast(I32).rearrange("p (l e) -> p l e", l=3),
-                picked[rows, :, HALF * h : HALF * (h + 1)].bitcast(I32),
+                planes[a, first][r:P:32].bitcast(I32), picked[rows, :, HALF * first : HALF * (first + count)].bitcast(I32)
             )
 
         nc.sync.dma_start(tab_rows[ROW0:, :].bitcast(I32), tab_scales.rearrange("a q t -> (a q) t").bitcast(I32))
@@ -98,18 +99,18 @@ def tile_list_guess_floor_mastery_kernel(
         load_wa(0)
         for r in range(4):
             load_w_rows(0, r)
-        nc.sync.dma_start(wq_raw[:], wq_words.rearrange("a p e -> p a e").bitcast(I32))
         load_wa(1)
 
         for l in range(3):
             nc.vector.tensor_copy(picked[:, l, :], tab_rows[:].indirect(lists[l][:]))
         sort_w_rows(0)
         for r in range(4):
-            move_plane(0, 0, r)
+            move_plane(0, 0, 2, r)
         tab.append(held([P, T], I32, "tab1", "tab_rows"))
         load_tab(1)
+        nc.sync.dma_start(wq_raw[:], wq_words.rearrange("a p e -> p a e").bitcast(I32))
         for r in range(4):
-            move_plane(0, 1, r)
+            move_plane(1, 0, 1, r)
         nc.sync.dma_start(wg_raw[:], wg_words.rearrange("a p e i -> p a (e i)").bitcast(I32))
         for r in range(4):
             load_w_rows(1, r)
@@ -117,11 +118,9 @@ def tile_list_guess_floor_mastery_kernel(
         nc.sync.dma_start(bo_sb[:], bo.rearrange("(g p t) -> p g t", g=GROUPS, t=4))
         load_wo(0)
         nc.sync.dma_start(gain_raw[:], gain.rearrange("(p t) -> p t", t=4))
-        for r in range(4):
-            move_plane(1, 1, r)
         load_wo(1)
         for r in range(4):
-            move_plane(1, 0, r)
+            move_plane(1, 1, 1, r)
 
         words = {}
 
@@ -189,20 +188,21 @@ def tile_list_guess_floor_mastery_kernel(
 
         def moving(l, a, w):
             h, v = divmod(w, HALF // STRIP)
-            first = l * HALF + v * STRIP
-            return words[l, a, h][:, v * STRIP : (v + 1) * STRIP].bitcast(FP8X4), planes[h][a][:, first : first + STRIP]
+            plane, first = (planes[1, h], v * STRIP) if a else (planes[0, 0], w * STRIP)
+            return words[l, a, h][:, v * STRIP : (v + 1) * STRIP].bitcast(FP8X4), plane[:, l, first : first + STRIP]
 
         success = {}
 
         def difference(w, u):
             diff = psum.tile([P, 2, STRIP], F32, name="diff", tag="bank%d" % ((2 * w + u) % 4))
-            for a in range(PASSES):
+            order = (0, 1) if w < 2 else (1, 0)
+            for a in order:
                 for i in range(2):
                     m = slice(128 * (2 * u + i), 128 * (2 * u + i + 1))
                     nc.tensor.matmul_mx(
                         diff[:, i, :], lhsT=wa_codes[:, a, m].bitcast(FP8X4), lhsT_scale=wa_planes[:, a, m],
                         rhs=moving(0, a, w)[0], rhs_scale=moving(0, a, w)[1],
-                        start=(a == 0 and i == 0), stop=False,
+                        start=(a == order[0] and i == 0), stop=False,
                     )
                 for i in range(2):
                     t = 2 * u + i
@@ -210,20 +210,20 @@ def tile_list_guess_floor_mastery_kernel(
                         diff[:, i, :], lhsT=wq_codes[:, a, 256 * t : 256 * (t + 1)].bitcast(FP4X4),
                         lhsT_scale=w_planes[0][:, a, 128 * t : 128 * (t + 1)],
                         rhs=moving(1, a, w)[0], rhs_scale=moving(1, a, w)[1],
-                        start=False, stop=(a == PASSES - 1 and i == 1),
+                        start=False, stop=(a == order[1] and i == 1),
                     )
             success[w, u] = held([P, STRIP, 2], F32, "success%d%d" % (w, u))
             nc.scalar.activation(success[w, u][:], diff[:].rearrange("p i n -> p n i"), ACT.Sigmoid, scale=-1.0)
 
         def guess_floor(w, u, larger):
             guess = psum.tile([P, 2, STRIP], F32, name="guess", tag="bank%d" % (4 + (2 * w + u) % 4))
-            for a in range(PASSES):
+            for a in reversed(range(PASSES)):
                 for i in range(2):
                     m = slice(128 * (2 * u + i), 128 * (2 * u + i + 1))
                     nc.tensor.matmul_mx(
                         guess[:, i, :], lhsT=wg_codes[u][:, a, 128 * i : 128 * (i + 1)].bitcast(FP8X4), lhsT_scale=w_planes[1][:, a, m],
                         rhs=moving(2, a, w)[0], rhs_scale=moving(2, a, w)[1],
-                        start=(a == 0 and i == 0), stop=(a == PASSES - 1 and i == 1),
+                        start=(a == PASSES - 1 and i == 0), stop=(a == 0 and i == 1),
                     )
             nc.vector.tensor_tensor(larger[:, u], guess[:].rearrange("p i n -> p n i"), success[w, u][:], ALU.max)
 

@@ -42,7 +42,7 @@ def tile_list_guess_floor_mastery_kernel(
             return keep.tile(shape, dtype, name=name, tag=tag or name, align_bytes=64)
 
         lists = [held([P, S // 16], U16, "list%d" % l) for l in range(3)]
-        tab = [held([P, T], I32, "tab0")]
+        tab = [held([P, T], I32, "tab%d" % a) for a in range(PASSES)]
         tab_rows = held([P, T], U8, "tab_rows")
         w_rows = [held([P, PASSES, H], U8, "w_rows%d" % i) for i in range(2)]
         w_planes = [held([P, PASSES, H], U8, "w_planes%d" % i) for i in range(2)]
@@ -100,14 +100,13 @@ def tile_list_guess_floor_mastery_kernel(
         for r in range(4):
             load_w_rows(0, r)
         load_wa(1)
+        load_tab(1)
 
         for l in range(3):
             nc.vector.tensor_copy(picked[:, l, :], tab_rows[:].indirect(lists[l][:]))
         sort_w_rows(0)
         for r in range(4):
             move_plane(0, 0, 2, r)
-        tab.append(held([P, T], I32, "tab1", "tab_rows"))
-        load_tab(1)
         nc.sync.dma_start(wq_raw[:], wq_words.rearrange("a p e -> p a e").bitcast(I32))
         for r in range(4):
             move_plane(1, 0, 1, r)

from contextlib import ExitStack

import concourse.mybir as mybir

K, T, S, H, N = 1024, 4096, 1024, 512, 1024
FLOPS = 2 * S * H * (3 * K + N)

F32 = mybir.dt.float32
BF16 = mybir.dt.bfloat16
I32 = mybir.dt.int32
U32 = mybir.dt.uint32
U16 = mybir.dt.uint16
U8 = mybir.dt.uint8
FP8X4 = mybir.dt.float8_e4m3fn_x4
FP4X4 = mybir.dt.float4_e2m1fn_x4
ACT = mybir.ActivationFunctionType
ALU = mybir.AluOpType

P = 128
PASSES = K // 512
GROUPS = N // 512
HALF = 512
ROW0 = 96
STRIP = 256
STRIPS = S // STRIP
CHUNK = 128
ROUND_BEHIND = {(0, 0): "wo_bf1", (0, 1): "h_bf"}
Y_ORDER = [(0, 0), (0, 1), (1, 0), (1, 1), (2, 0), (2, 1), (3, 0), (3, 1)]
LOGIT_BANKS = (0, 1, 0, 1, 2, 3, 4, 5, 0, 1, 6, 7, 2, 3, 4, 5)


def tile_list_guess_floor_mastery_kernel(
    tc, tab_words, tab_scales, offs, offs2, offs3, wa, wq_words, wq_scales, wg_words, wg_scales,
    gain, wo, bo, out_0, out_1, out_2,
):
    nc = tc.nc
    with ExitStack() as ctx:
        keep = ctx.enter_context(tc.tile_pool(name="keep", bufs=1))
        psum = ctx.enter_context(tc.psum_pool(name="psum", bufs=1))

        def held(shape, dtype, name, tag=None):
            return keep.tile(shape, dtype, name=name, tag=tag or name, align_bytes=64)

        lists = [held([P, S // 16], U16, "list%d" % l) for l in range(3)]
        tab = [held([P, T], I32, "tab%d" % a) for a in range(PASSES)]
        tab_rows = held([P, T], U8, "tab_rows")
        w_rows = [held([P, PASSES, H], U8, "w_rows%d" % i) for i in range(2)]
        w_planes = [held([P, PASSES, H], U8, "w_planes%d" % i) for i in range(2)]
        planes = {
            (a, first): held([P, 3, count * HALF], U8, "planes%d%d" % (a, first))
            for a, first, count in ((0, 0, 2), (1, 0, 1), (1, 1, 1))
        }
        wa_raw = [held([P, 4, H], F32, "wa_raw%d" % a) for a in range(PASSES)]
        wo_raw = [held([P, 4, 512], F32, "wo_raw%d" % g) for g in range(GROUPS)]
        picked = held([P, 3, S], U8, "picked")
        wq_raw = held([P, PASSES, H // 2], I32, "wq_raw")
        wg_raw = held([P, PASSES, H], I32, "wg_raw")
        gain_sb = held([P, CHUNK * 4], F32, "gain_sb")
        gain_raw = held([P, 4], F32, "gain_raw")
        bo_sb = held([P, GROUPS, 4], F32, "bo_sb")

        for i in range(2):
            nc.gpsimd.memset(w_rows[i][:].rearrange("p a e -> p (a e)").bitcast(I32), 0)
        nc.vector.memset(tab_rows[0:ROW0, :].bitcast(I32), 0)
        for (a, first), plane in planes.items():
            (nc.vector, nc.gpsimd)[a].memset(plane[:].rearrange("p l e -> p (l e)").bitcast(I32), 0)

        def load_tab(a):
            nc.sync.dma_start(tab[a][:], tab_words[a].rearrange("p t i -> p (t i)").bitcast(I32))

        def load_wa(a):
            nc.sync.dma_start(wa_raw[a][:], wa[512 * a : 512 * (a + 1), :].rearrange("(p j) r -> p j r", j=4))

        def load_wo(g):
            nc.sync.dma_start(wo_raw[g][:], wo[:, 512 * g : 512 * (g + 1)].rearrange("(p j) n -> p j n", j=4))

        def load_w_rows(i, r):
            src = (wq_scales, wg_scales)[i]
            nc.sync.dma_start(
                w_rows[i][r:P:32].bitcast(I32), src[:, r:16:4, :].rearrange("a q e -> q a e").bitcast(I32)
            )

        def sort_w_rows(i):
            nc.gpsimd.tensor_copy(
                w_planes[i][:].rearrange("p a (t m) -> p a t m", t=4),
                w_rows[i][:].rearrange("p a (m t) -> p a t m", t=4),
            )

        def move_plane(a, first, count, r):
            rows = slice(ROW0 + 16 * a + r, ROW0 + 16 * (a + 1), 4)
            nc.sync.dma_start(
                planes[a, first][r:P:32].bitcast(I32), picked[rows, :, HALF * first : HALF * (first + count)].bitcast(I32)
            )

        nc.sync.dma_start(tab_rows[ROW0:, :].bitcast(I32), tab_scales.rearrange("a q t -> (a q) t").bitcast(I32))
        for l, src in enumerate((offs, offs2, offs3)):
            nc.sync.dma_start(lists[l][:], src)
        load_tab(0)
        load_wa(0)
        for r in range(4):
            load_w_rows(0, r)
        load_wa(1)
        load_tab(1)

        for l in range(3):
            nc.vector.tensor_copy(picked[:, l, :], tab_rows[:].indirect(lists[l][:]))
        sort_w_rows(0)
        for r in range(4):
            move_plane(0, 0, 2, r)
        nc.sync.dma_start(wq_raw[:], wq_words.rearrange("a p e -> p a e").bitcast(I32))
        for r in range(4):
            move_plane(1, 0, 1, r)
        nc.sync.dma_start(wg_raw[:], wg_words.rearrange("a p e i -> p a (e i)").bitcast(I32))
        for r in range(4):
            load_w_rows(1, r)
        sort_w_rows(1)
        nc.sync.dma_start(bo_sb[:], bo.rearrange("(g p t) -> p g t", g=GROUPS, t=4))
        load_wo(0)
        nc.sync.dma_start(gain_raw[:], gain.rearrange("(p t) -> p t", t=4))
        load_wo(1)
        for r in range(4):
            move_plane(1, 1, 1, r)

        words = {}

        def gather(l, a, first, count, tag=None):
            room = held([P, count * HALF], U32, "room%d%d%d" % (l, a, first), tag)
            cols = slice(first * HALF // 16, (first + count) * HALF // 16)
            nc.vector.tensor_copy(room[:], tab[a][:].bitcast(U32).indirect(lists[l][:, cols]))
            for i in range(count):
                words[l, a, first + i] = room[:, i * HALF : (i + 1) * HALF]

        for l in range(2):
            gather(l, 0, 0, 2)

        wa_codes = held([P, PASSES, H], U32, "wa_codes")
        wa_planes = held([P, PASSES, H], U8, "wa_planes")
        for a in range(PASSES):
            wa_bf = held([P, 4, 128, 4], BF16, "wa_bf%d" % a)
            dst = wa_bf[:].rearrange("p (u i) m j -> p u m j i", i=2)
            src = wa_raw[a][:].rearrange("p j (m u i) -> p u m j i", u=2, i=2)
            for u in range(2):
                nc.scalar.activation(dst[:, u], src[:, u], ACT.Copy, scale=-1.0)
            nc.vector.quantize_mx(
                wa_codes[:, a, :].bitcast(FP8X4), wa_planes[:, a, :], wa_bf[:].rearrange("p t m j -> p (t m j)")
            )
            if a == 0:
                gather(2, 0, 0, 2, "wa_bf0")

        wq_codes = held([P, PASSES, 2 * H], U8, "wq_codes")
        wg_codes = [held([P, PASSES, H // 2], I32, "wg_codes%d" % u) for u in range(2)]
        nc.scalar.copy(
            wq_codes[:].bitcast(U16).rearrange("p a (u i m) -> p a u m i", u=2, i=2),
            wq_raw[:].bitcast(U16).rearrange("p a (m u i) -> p a u m i", u=2, i=2),
        )
        for u in range(2):
            nc.gpsimd.tensor_copy(
                wg_codes[u][:].rearrange("p a (i m) -> p a i m", i=2),
                wg_raw[:].rearrange("p a (m t) -> p a t m", t=4)[:, :, 2 * u : 2 * u + 2],
            )
        for h in range(2):
            for l in range(3 - h):
                gather(l, 1, h, 1)
        nc.gpsimd.tensor_copy(
            gain_sb[:].rearrange("p (n t) -> p n t", t=4), gain_raw[:].unsqueeze(1).to_broadcast([P, CHUNK, 4])
        )

        wo_codes = {}
        wo_planes = held([P, GROUPS, 512], U8, "wo_planes")

        def quantize_wo(g):
            wo_bf = held([P, 4, 128, 4], BF16, "wo_bf%d" % g)
            dst = wo_bf[:].rearrange("p (u i) m j -> p u m j i", i=2)
            src = wo_raw[g][:].rearrange("p j (m u i) -> p u m j i", u=2, i=2)
            for m in range(0, 128, 64):
                for u in range(2):
                    nc.scalar.copy(dst[:, u, m : m + 64], src[:, u, m : m + 64])
            wo_codes[g] = held([P, 512], U32, "wo_codes%d" % g, (None, "larger1")[g])
            nc.vector.quantize_mx(
                wo_codes[g][:].bitcast(FP8X4), wo_planes[:, g, :], wo_bf[:].rearrange("p t m j -> p (t m j)")
            )

        y_codes = held([P, GROUPS, S], I32, "y_codes")
        y_planes = held([P, GROUPS, S], U8, "y_planes")
        out_rows = out_0.rearrange("(g p t) j -> g p t j", g=GROUPS, t=4)
        out_words = out_1.rearrange("g p m i -> p g (m i)").bitcast(I32)

        def moving(l, a, w):
            h, v = divmod(w, HALF // STRIP)
            plane, first = (planes[1, h], v * STRIP) if a else (planes[0, 0], w * STRIP)
            return words[l, a, h][:, v * STRIP : (v + 1) * STRIP].bitcast(FP8X4), plane[:, l, first : first + STRIP]

        success = {}

        def difference(w, u):
            diff = psum.tile([P, 2, STRIP], F32, name="diff", tag="bank%d" % ((2 * w + u) % 4))
            order = (0, 1) if w < 2 else (1, 0)
            for a in order:
                for i in range(2):
                    m = slice(128 * (2 * u + i), 128 * (2 * u + i + 1))
                    nc.tensor.matmul_mx(
                        diff[:, i, :], lhsT=wa_codes[:, a, m].bitcast(FP8X4), lhsT_scale=wa_planes[:, a, m],
                        rhs=moving(0, a, w)[0], rhs_scale=moving(0, a, w)[1],
                        start=(a == order[0] and i == 0), stop=False,
                    )
                for i in range(2):
                    t = 2 * u + i
                    nc.tensor.matmul_mx(
                        diff[:, i, :], lhsT=wq_codes[:, a, 256 * t : 256 * (t + 1)].bitcast(FP4X4),
                        lhsT_scale=w_planes[0][:, a, 128 * t : 128 * (t + 1)],
                        rhs=moving(1, a, w)[0], rhs_scale=moving(1, a, w)[1],
                        start=False, stop=(a == order[1] and i == 1),
                    )
            success[w, u] = held([P, STRIP, 2], F32, "success%d%d" % (w, u))
            nc.scalar.activation(success[w, u][:], diff[:].rearrange("p i n -> p n i"), ACT.Sigmoid, scale=-1.0)

        def guess_floor(w, u, larger):
            guess = psum.tile([P, 2, STRIP], F32, name="guess", tag="bank%d" % (4 + (2 * w + u) % 4))
            for a in reversed(range(PASSES)):
                for i in range(2):
                    m = slice(128 * (2 * u + i), 128 * (2 * u + i + 1))
                    nc.tensor.matmul_mx(
                        guess[:, i, :], lhsT=wg_codes[u][:, a, 128 * i : 128 * (i + 1)].bitcast(FP8X4), lhsT_scale=w_planes[1][:, a, m],
                        rhs=moving(2, a, w)[0], rhs_scale=moving(2, a, w)[1],
                        start=(a == PASSES - 1 and i == 0), stop=(a == 0 and i == 1),
                    )
            nc.vector.tensor_tensor(larger[:, u], guess[:].rearrange("p i n -> p n i"), success[w, u][:], ALU.max)

        larger, h_bf, h_mx = {}, {}, {}

        def maxima(w):
            larger[w] = held([P, 2, STRIP, 2], F32, "larger%d" % w, ("larger0", "larger1", "larger0", "wo_bf1")[w])
            for u in range(2):
                guess_floor(w, u, larger[w])

        def times_gain(w, c, engine):
            if w not in h_bf:
                h_bf[w] = held([P, STRIP // CHUNK, CHUNK, 2, 2], BF16, "h_bf%d" % w, "h_bf")
            engine.tensor_tensor(
                h_bf[w][:, c],
                larger[w][:, :, CHUNK * c : CHUNK * (c + 1), :].rearrange("p u n i -> p n u i"),
                gain_sb[:].rearrange("p (n u i) -> p n u i", u=2, i=2),
                ALU.mult,
            )

        def quantize_h(w):
            h_codes = held([P, STRIP], U32, "h_codes%d" % w)
            h_planes = held([P, STRIP], U8, "h_planes%d" % w)
            nc.vector.quantize_mx(
                h_codes[:].bitcast(FP8X4), h_planes[:], h_bf[w][:].rearrange("p c n u i -> p (c n u i)")
            )
            h_mx[w] = (h_codes, h_planes)

        ys = {}

        def second_stage(w, g):
            h, v = divmod(w, HALF // STRIP)
            cols = slice(v * STRIP, (v + 1) * STRIP)
            h_codes, h_planes = h_mx[w]
            if (h, g) not in ys:
                ys[h, g] = held([P, 4, HALF], F32, "y%d%d" % (h, g))
            y = ys[h, g]
            for pair in range(2):
                bank = LOGIT_BANKS[2 * Y_ORDER.index((w, g)) + pair]
                logits = psum.tile([P, 2, STRIP], F32, name="logits", tag="bank%d" % bank)
                for e in range(2):
                    m = slice(128 * (2 * pair + e), 128 * (2 * pair + e + 1))
                    nc.tensor.matmul_mx(
                        logits[:, e, :], lhsT=wo_codes[g][:, m].bitcast(FP8X4), lhsT_scale=wo_planes[:, g, m],
                        rhs=h_codes[:].bitcast(FP8X4), rhs_scale=h_planes[:], start=True, stop=True,
                    )
                for e in range(2):
                    t = 2 * pair + e
                    nc.scalar.activation(y[:, t, cols], logits[:, e, :], ACT.Identity, bias=bo_sb[:, g, t : t + 1])
            nc.sync.dma_start(out_rows[g][:, :, w * STRIP : (w + 1) * STRIP], y[:, :, cols])

        y_bf = {}

        def round_y(engine_copy, h, g, first, count):
            if (h, g) not in y_bf:
                y_bf[h, g] = held([P, HALF, 4], BF16, "y_bf%d%d" % (h, g), ROUND_BEHIND.get((h, g)))
            cols = slice(first * STRIP, (first + count) * STRIP)
            engine_copy(
                y_bf[h, g][:, cols].rearrange("p (c i) t -> p c t i", i=2),
                ys[h, g][:, :, cols].rearrange("p t (c i) -> p c t i", i=2),
            )

        def quantize_y(h, g, first, count):
            cols = slice(first * STRIP, (first + count) * STRIP)
            out_cols = slice(h * HALF + first * STRIP, h * HALF + (first + count) * STRIP)
            nc.vector.quantize_mx(
                y_codes[:, g, out_cols].bitcast(FP8X4), y_planes[:, g, out_cols],
                y_bf[h, g][:, cols].rearrange("p n t -> p (n t)"),
            )

        for w in range(2):
            for u in range(2):
                difference(w, u)
        maxima(0)
        for c in range(2):
            times_gain(0, c, nc.gpsimd)
        gather(2, 1, 1, 1, "success01")
        maxima(1)
        quantize_wo(0)
        quantize_h(0)
        for w in range(1, STRIPS - 1):
            times_gain(w, 0, nc.gpsimd)
            for u in range(2):
                difference(w + 1, u)
            maxima(w + 1)
            times_gain(w, 1, nc.vector)
            if w == 1:
                quantize_wo(1)
            quantize_h(w)
            for g in range(GROUPS):
                second_stage(w - 1, g)
        for c in range(2):
            times_gain(STRIPS - 1, c, nc.vector)
        quantize_h(STRIPS - 1)
        for w, g in Y_ORDER[4:]:
            second_stage(w, g)
        for g in range(GROUPS):
            round_y(nc.vector.tensor_copy, 0, g, 0, 2)
        for g in range(GROUPS):
            quantize_y(0, g, 0, 2)
        nc.sync.dma_start(out_words[:, :, :HALF], y_codes[:, :, :HALF])
        round_y(nc.vector.tensor_copy, 1, 0, 0, 2)
        quantize_y(1, 0, 0, 2)
        nc.sync.dma_start(out_words[:, 0, HALF:], y_codes[:, 0, HALF:])
        round_y(nc.scalar.copy, 1, 1, 0, 1)
        round_y(nc.vector.tensor_copy, 1, 1, 1, 1)
        for v in (1, 0):
            quantize_y(1, 1, v, 1)
            cols = slice(HALF + v * STRIP, HALF + (v + 1) * STRIP)
            nc.sync.dma_start(out_words[:, 1, cols], y_codes[:, 1, cols])

        for r in range(4):
            (nc.sync, nc.scalar)[r % 2].dma_start(
                out_2[:, r:16:4, :].rearrange("g q m -> q g m").bitcast(I32), y_planes[r:P:32].bitcast(I32)
            )
